import numpy as np
import ml_dtypes


def mxq(x, axis, fmt="e4m3"):
    dtype, down = {"e4m3": (ml_dtypes.float8_e4m3fn, 7), "e5m2": (ml_dtypes.float8_e5m2, 14)}[fmt]
    v = np.moveaxis(np.asarray(x, np.float32).astype(ml_dtypes.bfloat16).astype(np.float64), axis, -1)
    blocks = v.reshape(v.shape[:-1] + (-1, 32))
    amax = np.abs(blocks).max(-1, keepdims=True)
    byte = np.maximum(np.where(amax > 0, np.frexp(amax)[1] - 1 + 127, 0) - down, 1)
    scale = np.exp2(byte - 127.0)
    codes = (blocks / scale).astype(np.float32).astype(dtype).astype(np.float64)
    return np.moveaxis((codes * scale).reshape(v.shape), -1, axis)


WIDE = False


def mx_kscale(k):
    if not WIDE:
        return np.ones(k)
    levels = np.array([10, -10, 5, -5, 0])
    if k % 512:
        return np.exp2(np.random.permutation(np.resize(levels, k // 32))).repeat(32)
    a = np.empty((k // 512, 16))
    for p in range(k // 512):
        a[p, :8] = np.random.permutation(np.resize(levels, 8))
        for g in range(8):
            far = levels[np.abs(levels - a[p, g]) >= 10]
            a[p, g + 8] = far[np.random.randint(len(far))]
    return np.exp2(a.ravel()).repeat(32)


def f64(x):
    return np.asarray(x).astype(np.float64)


def striped8(idx):
    return np.concatenate([x.reshape(-1, 16).T for x in idx]).astype(np.uint16)


def runs(offs, k):
    lists = np.stack([offs[16 * r : 16 * r + 16].T.reshape(-1) for r in range(8)]).astype(np.int64)
    return lists[np.arange(k) % 512 // 64]


def pack_weight(w):
    k, n = w.shape
    w = f64(np.asarray(w, np.float32).astype(ml_dtypes.bfloat16)).reshape(k // 32, 32, n)
    amax = np.abs(w).max(1)
    byte = np.clip(np.where(amax > 0, np.frexp(amax)[1] - 1 + 127 - 7, 1), 1, 254)
    scaled = (w * np.exp2(127.0 - byte)[:, None, :]).reshape(k, n).astype(np.float32)
    words = np.ascontiguousarray(scaled.reshape(k // 512, 128, 4, n).transpose(0, 1, 3, 2)).astype(ml_dtypes.float8_e4m3fn).view(np.uint8)
    return words, np.ascontiguousarray(byte.astype(np.uint8).reshape(k // 512, 16, n))


def unpack_weight(words, scales):
    g, p, n, _ = words.shape
    vals = np.ascontiguousarray(words).view(ml_dtypes.float8_e4m3fn).astype(np.float64) * np.repeat(np.exp2(scales.astype(np.float64) - 127.0), 8, axis=1)[..., None]
    return vals.transpose(0, 1, 3, 2).reshape(g * 512, n)


K, T, S, H, N = 512, 2048, 512, 512, 128


def setup_inputs():
    n = np.random.standard_normal
    s = mx_kscale(K)[:, None]
    u = mx_kscale(H)
    packed_xT = pack_weight(n((K, T)) * s)
    packed_w1 = pack_weight(n((K, N)) / np.sqrt(2 * K) / s)
    packed_w3 = pack_weight(n((H, N)) / np.sqrt(2 * H) / u[:, None])
    return {
        "x_words": packed_xT[0],
        "x_scales": packed_xT[1],
        "w1_words": packed_w1[0],
        "w1_scales": packed_w1[1],
        "w2": (n((K, H)) / np.sqrt(K) / s * u).astype(np.float32),
        "w3_words": packed_w3[0],
        "w3_scales": packed_w3[1],
        "offs": striped8(np.stack([np.random.permutation(T)[:S] for _ in range(8)])),
    }


def reference(x_words, x_scales, w1_words, w1_scales, w2, w3_words, w3_scales, offs):
    xq = unpack_weight(x_words, x_scales)[np.arange(K)[:, None], runs(offs, K)]
    h = mxq(f64(w2), 0, "e4m3").T @ xq
    return unpack_weight(w1_words, w1_scales).T @ xq + unpack_weight(w3_words, w3_scales).T @ mxq(h, 0, "e4m3")

@@ -1,0 +1,145 @@
+from contextlib import ExitStack
+
+import concourse.mybir as mybir
+
+K, T, S, H, N = 512, 2048, 512, 512, 128
+FLOPS = 2 * K * H * S + 2 * K * N * S + 2 * H * N * S
+
+F32 = mybir.dt.float32
+BF16 = mybir.dt.bfloat16
+I32 = mybir.dt.int32
+U32 = mybir.dt.uint32
+U16 = mybir.dt.uint16
+U8 = mybir.dt.uint8
+FP8X4 = mybir.dt.float8_e4m3fn_x4
+
+P = 128
+PACK = 4
+CHUNK = 128
+HALF = 256
+
+
+def tile_picked_phlora_none_p_kernel(
+    tc, x_words, x_scales, w1_words, w1_scales, w2, w3_words, w3_scales, offs, out
+):
+    nc = tc.nc
+    with ExitStack() as ctx:
+        keep = ctx.enter_context(tc.tile_pool(name="keep", bufs=1))
+        psum = ctx.enter_context(tc.psum_pool(name="psum", bufs=1))
+
+        offsets = keep.tile([P, S // 16], U16, name="offsets")
+        nc.sync.dma_start(offsets[:], offs)
+
+        x_table = keep.tile([P, T], I32, name="x_table", align_bytes=64)
+        nc.scalar.dma_start(x_table[:], x_words[0].rearrange("p c r -> p (c r)").bitcast(I32))
+        w2_rows = w2.rearrange("(p j) c -> p j c", j=PACK)
+        w2_raw = []
+        for a in range(2):
+            raw = keep.tile([P, PACK, H // 2], F32, name=f"w2_raw{a}")
+            nc.scalar.dma_start(raw[:], w2_rows[:, :, a * H // 2 : (a + 1) * H // 2])
+            w2_raw.append(raw)
+
+        s_table = keep.tile([P, T], U8, name="s_table", align_bytes=64)
+        nc.vector.memset(s_table[:].bitcast(I32), 0)
+        nc.sync.dma_start(s_table[0:P:8, :].bitcast(I32), x_scales[0].bitcast(I32))
+
+        planes = keep.tile([P, S + 2 * N], U8, name="planes", align_bytes=64)
+        nc.vector.memset(planes[:, S : S + 2 * N].bitcast(I32), 0)
+        nc.sync.dma_start(planes[0:P:8, S : S + N].bitcast(I32), w1_scales[0].bitcast(I32))
+        nc.sync.dma_start(planes[0:P:8, S + N : S + 2 * N].bitcast(I32), w3_scales[0].bitcast(I32))
+
+        w1_codes = keep.tile([P, N], I32, name="w1_codes", align_bytes=64)
+        w3_codes = keep.tile([P, N], I32, name="w3_codes", align_bytes=64)
+        nc.gpsimd.dma_start(w1_codes[:], w1_words[0].rearrange("p c r -> p (c r)").bitcast(I32))
+        nc.gpsimd.dma_start(w3_codes[:], w3_words[0].rearrange("p c r -> p (c r)").bitcast(I32))
+
+        s_picked = keep.tile([P, S], U8, name="s_picked", tag="picked0", align_bytes=64)
+        nc.vector.tensor_copy(s_picked[:], s_table[:].indirect(offsets[:]))
+        nc.vector.tensor_copy(planes[:, 0:S], s_picked[:])
+        for i in range(1, 4):
+            nc.sync.dma_start(planes[i:P:32, :].bitcast(I32), planes[8 * i : P : 32, :].bitcast(I32))
+
+        x_picked = []
+        for a in range(S // HALF):
+            xp = keep.tile([P, HALF], U32, name=f"x_picked{a}", tag=f"picked{a}", align_bytes=64)
+            nc.vector.tensor_copy(
+                xp[:], x_table[:].bitcast(U32).indirect(offsets[:, a * HALF // 16 : (a + 1) * HALF // 16])
+            )
+            x_picked.append(xp)
+
+        w2_codes = keep.tile([P, H], U32, name="w2_codes", align_bytes=64)
+        w2_plane = keep.tile([P, H], U8, name="w2_plane", align_bytes=64)
+        for a in range(2):
+            src = w2_raw[a][:].rearrange("p j (m t) -> p m j t", t=PACK)
+            for u, copy in enumerate((nc.vector.tensor_copy, nc.scalar.copy)):
+                w2_bf = keep.tile([P, 2 * HALF], BF16, name=f"w2_bf{a}{u}", align_bytes=64)
+                copy(w2_bf[:].rearrange("p (t m j) -> p m j t", t=2, j=PACK), src[:, :, :, 2 * u : 2 * u + 2])
+                for e in range(2):
+                    lo = (2 * u + e) * P + a * P // 2
+                    nc.vector.quantize_mx(
+                        out=w2_codes[:, lo : lo + P // 2].bitcast(FP8X4),
+                        scales=w2_plane[:, lo : lo + P // 2],
+                        in_=w2_bf[:, e * HALF : (e + 1) * HALF],
+                    )
+
+        def x_operand(c):
+            lo = c * CHUNK % HALF
+            return x_picked[c * CHUNK // HALF][:, lo : lo + CHUNK].bitcast(FP8X4), planes[:, c * CHUNK : (c + 1) * CHUNK]
+
+        chunks = S // CHUNK
+        accs = []
+        for c in range(chunks):
+            codes, plane = x_operand(c)
+            acc = psum.tile([P, CHUNK], F32, name=f"acc{c}")
+            nc.tensor.matmul_mx(
+                out=acc[:],
+                lhsT=w1_codes[:].bitcast(FP8X4),
+                lhsT_scale=planes[:, S : S + N],
+                rhs=codes,
+                rhs_scale=plane,
+                start=True,
+                stop=False,
+            )
+            accs.append(acc)
+
+        h_banks = []
+        for c in range(chunks):
+            codes, plane = x_operand(c)
+            bank = psum.tile([P, PACK, CHUNK], F32, name=f"h_bank{c}")
+            for t in range(PACK):
+                nc.tensor.matmul_mx(
+                    out=bank[:, t, :],
+                    lhsT=w2_codes[:, t * P : (t + 1) * P].bitcast(FP8X4),
+                    lhsT_scale=w2_plane[:, t * P : (t + 1) * P],
+                    rhs=codes,
+                    rhs_scale=plane,
+                    start=True,
+                    stop=True,
+                )
+            h_banks.append(bank)
+
+        for c in range(chunks):
+            h_bf = keep.tile([P, CHUNK * PACK], BF16, name=f"h_bf{c}", align_bytes=64)
+            h_dst = h_bf[:].rearrange("p (n t) -> p n t", t=PACK)
+            h_src = h_banks[c][:].rearrange("p t n -> p n t")
+            if c == 1:
+                nc.vector.tensor_copy(h_dst, h_src)
+            else:
+                nc.scalar.copy(h_dst, h_src)
+            h_codes = keep.tile([P, CHUNK], U32, name=f"h_codes{c}", align_bytes=64)
+            h_plane = keep.tile([P, CHUNK], U8, name=f"h_plane{c}", align_bytes=64)
+            nc.vector.quantize_mx(out=h_codes[:].bitcast(FP8X4), scales=h_plane[:], in_=h_bf[:])
+
+            acc = accs[c]
+            nc.tensor.matmul_mx(
+                out=acc[:],
+                lhsT=w3_codes[:].bitcast(FP8X4),
+                lhsT_scale=planes[:, S + N : S + 2 * N],
+                rhs=h_codes[:].bitcast(FP8X4),
+                rhs_scale=h_plane[:],
+                start=False,
+                stop=True,
+            )
+            result = keep.tile([P, CHUNK], F32, name=f"result{c}")
+            nc.vector.tensor_copy(result[:], acc[:])
+            nc.sync.dma_start(out[:, c * CHUNK : (c + 1) * CHUNK], result[:])

@@ -30,14 +30,9 @@ def tile_picked_phlora_none_p_kernel(
         offsets = keep.tile([P, S // 16], U16, name="offsets")
         nc.sync.dma_start(offsets[:], offs)
 
+        x_rows = x_words[0].rearrange("p c r -> p (c r)").bitcast(I32)
         x_table = keep.tile([P, T], I32, name="x_table", align_bytes=64)
-        nc.scalar.dma_start(x_table[:], x_words[0].rearrange("p c r -> p (c r)").bitcast(I32))
-        w2_rows = w2.rearrange("(p j) c -> p j c", j=PACK)
-        w2_raw = []
-        for a in range(2):
-            raw = keep.tile([P, PACK, H // 2], F32, name=f"w2_raw{a}")
-            nc.scalar.dma_start(raw[:], w2_rows[:, :, a * H // 2 : (a + 1) * H // 2])
-            w2_raw.append(raw)
+        nc.sync.dma_start(x_table[:, 0:512], x_rows[:, 0:512])
 
         s_table = keep.tile([P, T], U8, name="s_table", align_bytes=64)
         nc.vector.memset(s_table[:].bitcast(I32), 0)
@@ -45,63 +40,48 @@ def tile_picked_phlora_none_p_kernel(
 
         planes = keep.tile([P, S + 2 * N], U8, name="planes", align_bytes=64)
         nc.vector.memset(planes[:, S : S + 2 * N].bitcast(I32), 0)
-        nc.sync.dma_start(planes[0:P:8, S : S + N].bitcast(I32), w1_scales[0].bitcast(I32))
-        nc.sync.dma_start(planes[0:P:8, S + N : S + 2 * N].bitcast(I32), w3_scales[0].bitcast(I32))
+        nc.scalar.dma_start(planes[0:P:8, S : S + N].bitcast(I32), w1_scales[0].bitcast(I32))
+        nc.scalar.dma_start(planes[0:P:8, S + N : S + 2 * N].bitcast(I32), w3_scales[0].bitcast(I32))
+
+        w2_raw = keep.tile([P, PACK, H], F32, name="w2_raw")
+        nc.sync.dma_start(w2_raw[:], w2.rearrange("(p j) c -> p j c", j=PACK))
+        nc.sync.dma_start(x_table[:, 512:T], x_rows[:, 512:T])
 
         w1_codes = keep.tile([P, N], I32, name="w1_codes", align_bytes=64)
         w3_codes = keep.tile([P, N], I32, name="w3_codes", align_bytes=64)
-        nc.gpsimd.dma_start(w1_codes[:], w1_words[0].rearrange("p c r -> p (c r)").bitcast(I32))
-        nc.gpsimd.dma_start(w3_codes[:], w3_words[0].rearrange("p c r -> p (c r)").bitcast(I32))
+        nc.sync.dma_start(w1_codes[:], w1_words[0].rearrange("p c r -> p (c r)").bitcast(I32))
+        nc.sync.dma_start(w3_codes[:], w3_words[0].rearrange("p c r -> p (c r)").bitcast(I32))
 
-        s_picked = keep.tile([P, S], U8, name="s_picked", tag="picked0", align_bytes=64)
+        s_picked = keep.tile([P, S], U8, name="s_picked", align_bytes=64)
         nc.vector.tensor_copy(s_picked[:], s_table[:].indirect(offsets[:]))
-        nc.vector.tensor_copy(planes[:, 0:S], s_picked[:])
+        nc.vector.tensor_copy(planes[:, 0:S].bitcast(I32), s_picked[:].bitcast(I32))
         for i in range(1, 4):
             nc.sync.dma_start(planes[i:P:32, :].bitcast(I32), planes[8 * i : P : 32, :].bitcast(I32))
 
-        x_picked = []
-        for a in range(S // HALF):
-            xp = keep.tile([P, HALF], U32, name=f"x_picked{a}", tag=f"picked{a}", align_bytes=64)
-            nc.vector.tensor_copy(
-                xp[:], x_table[:].bitcast(U32).indirect(offsets[:, a * HALF // 16 : (a + 1) * HALF // 16])
-            )
-            x_picked.append(xp)
-
         w2_codes = keep.tile([P, H], U32, name="w2_codes", align_bytes=64)
         w2_plane = keep.tile([P, H], U8, name="w2_plane", align_bytes=64)
-        for a in range(2):
-            src = w2_raw[a][:].rearrange("p j (m t) -> p m j t", t=PACK)
-            for u, copy in enumerate((nc.vector.tensor_copy, nc.scalar.copy)):
-                w2_bf = keep.tile([P, 2 * HALF], BF16, name=f"w2_bf{a}{u}", align_bytes=64)
-                copy(w2_bf[:].rearrange("p (t m j) -> p m j t", t=2, j=PACK), src[:, :, :, 2 * u : 2 * u + 2])
-                for e in range(2):
-                    lo = (2 * u + e) * P + a * P // 2
-                    nc.vector.quantize_mx(
-                        out=w2_codes[:, lo : lo + P // 2].bitcast(FP8X4),
-                        scales=w2_plane[:, lo : lo + P // 2],
-                        in_=w2_bf[:, e * HALF : (e + 1) * HALF],
-                    )
+        w2_src = w2_raw[:].rearrange("p j (m t) -> p m j t", t=PACK)
+        for u, copy in enumerate((nc.vector.tensor_copy, nc.scalar.copy)):
+            w2_bf = keep.tile([P, 2 * H], BF16, name=f"w2_bf{u}", tag=f"slot{u}", align_bytes=64)
+            copy(w2_bf[:].rearrange("p (t m j) -> p m j t", t=2, j=PACK), w2_src[:, :, :, 2 * u : 2 * u + 2])
+            nc.vector.quantize_mx(
+                out=w2_codes[:, u * HALF : (u + 1) * HALF].bitcast(FP8X4),
+                scales=w2_plane[:, u * HALF : (u + 1) * HALF],
+                in_=w2_bf[:],
+            )
+
+        x_picked = keep.tile([P, S], U32, name="x_picked", tag="slot1", align_bytes=64)
+        for a in range(S // HALF):
+            nc.vector.tensor_copy(
+                x_picked[:, a * HALF : (a + 1) * HALF],
+                x_table[:].bitcast(U32).indirect(offsets[:, a * HALF // 16 : (a + 1) * HALF // 16]),
+            )
 
         def x_operand(c):
-            lo = c * CHUNK % HALF
-            return x_picked[c * CHUNK // HALF][:, lo : lo + CHUNK].bitcast(FP8X4), planes[:, c * CHUNK : (c + 1) * CHUNK]
+            cols = slice(c * CHUNK, (c + 1) * CHUNK)
+            return x_picked[:, cols].bitcast(FP8X4), planes[:, cols]
 
         chunks = S // CHUNK
-        accs = []
-        for c in range(chunks):
-            codes, plane = x_operand(c)
-            acc = psum.tile([P, CHUNK], F32, name=f"acc{c}")
-            nc.tensor.matmul_mx(
-                out=acc[:],
-                lhsT=w1_codes[:].bitcast(FP8X4),
-                lhsT_scale=planes[:, S : S + N],
-                rhs=codes,
-                rhs_scale=plane,
-                start=True,
-                stop=False,
-            )
-            accs.append(acc)
-
         h_banks = []
         for c in range(chunks):
             codes, plane = x_operand(c)
@@ -118,21 +98,30 @@ def tile_picked_phlora_none_p_kernel(
                 )
             h_banks.append(bank)
 
+        accs = []
+        for c in range(chunks):
+            codes, plane = x_operand(c)
+            acc = psum.tile([P, CHUNK], F32, name=f"acc{c}")
+            nc.tensor.matmul_mx(
+                out=acc[:],
+                lhsT=w1_codes[:].bitcast(FP8X4),
+                lhsT_scale=planes[:, S : S + N],
+                rhs=codes,
+                rhs_scale=plane,
+                start=True,
+                stop=False,
+            )
+            accs.append(acc)
+
         for c in range(chunks):
             h_bf = keep.tile([P, CHUNK * PACK], BF16, name=f"h_bf{c}", align_bytes=64)
-            h_dst = h_bf[:].rearrange("p (n t) -> p n t", t=PACK)
-            h_src = h_banks[c][:].rearrange("p t n -> p n t")
-            if c == 1:
-                nc.vector.tensor_copy(h_dst, h_src)
-            else:
-                nc.scalar.copy(h_dst, h_src)
+            h_copy = nc.vector.tensor_copy if c == 2 else nc.scalar.copy
+            h_copy(h_bf[:].rearrange("p (n t) -> p n t", t=PACK), h_banks[c][:].rearrange("p t n -> p n t"))
             h_codes = keep.tile([P, CHUNK], U32, name=f"h_codes{c}", align_bytes=64)
             h_plane = keep.tile([P, CHUNK], U8, name=f"h_plane{c}", align_bytes=64)
             nc.vector.quantize_mx(out=h_codes[:].bitcast(FP8X4), scales=h_plane[:], in_=h_bf[:])
-
-            acc = accs[c]
             nc.tensor.matmul_mx(
-                out=acc[:],
+                out=accs[c][:],
                 lhsT=w3_codes[:].bitcast(FP8X4),
                 lhsT_scale=planes[:, S + N : S + 2 * N],
                 rhs=h_codes[:].bitcast(FP8X4),
@@ -140,6 +129,9 @@ def tile_picked_phlora_none_p_kernel(
                 start=False,
                 stop=True,
             )
+
+        for c in range(chunks):
             result = keep.tile([P, CHUNK], F32, name=f"result{c}")
-            nc.vector.tensor_copy(result[:], acc[:])
+            out_copy = nc.vector.tensor_copy if c == chunks - 1 else nc.scalar.copy
+            out_copy(result[:], accs[c][:])
             nc.sync.dma_start(out[:, c * CHUNK : (c + 1) * CHUNK], result[:])

@@ -27,12 +27,12 @@ def tile_picked_phlora_none_p_kernel(
         keep = ctx.enter_context(tc.tile_pool(name="keep", bufs=1))
         psum = ctx.enter_context(tc.psum_pool(name="psum", bufs=1))
 
+        w2_rows = w2.rearrange("(p j) c -> p j c", j=PACK)
+        w2_raw = keep.tile([P, PACK, H], F32, name="w2_raw")
+        nc.sync.dma_start(w2_raw[:, 0:1, :], w2_rows[:, 0:1, :])
+
         offsets = keep.tile([P, S // 16], U16, name="offsets")
         nc.sync.dma_start(offsets[:], offs)
-
-        x_rows = x_words[0].rearrange("p c r -> p (c r)").bitcast(I32)
-        x_table = keep.tile([P, T], I32, name="x_table", align_bytes=64)
-        nc.sync.dma_start(x_table[:, 0:512], x_rows[:, 0:512])
 
         s_table = keep.tile([P, T], U8, name="s_table", align_bytes=64)
         nc.vector.memset(s_table[:].bitcast(I32), 0)
@@ -43,20 +43,24 @@ def tile_picked_phlora_none_p_kernel(
         nc.scalar.dma_start(planes[0:P:8, S : S + N].bitcast(I32), w1_scales[0].bitcast(I32))
         nc.scalar.dma_start(planes[0:P:8, S + N : S + 2 * N].bitcast(I32), w3_scales[0].bitcast(I32))
 
-        w2_raw = keep.tile([P, PACK, H], F32, name="w2_raw")
-        nc.sync.dma_start(w2_raw[:], w2.rearrange("(p j) c -> p j c", j=PACK))
-        nc.sync.dma_start(x_table[:, 512:T], x_rows[:, 512:T])
+        warm_in = keep.tile([P, 1], F32, name="warm_in")
+        warm_out = keep.tile([P, 1], F32, name="warm_out")
+        nc.gpsimd.memset(warm_in[:], 0.0)
+        nc.scalar.copy(warm_out[:], warm_in[:])
 
-        w1_codes = keep.tile([P, N], I32, name="w1_codes", align_bytes=64)
-        w3_codes = keep.tile([P, N], I32, name="w3_codes", align_bytes=64)
-        nc.sync.dma_start(w1_codes[:], w1_words[0].rearrange("p c r -> p (c r)").bitcast(I32))
-        nc.sync.dma_start(w3_codes[:], w3_words[0].rearrange("p c r -> p (c r)").bitcast(I32))
+        nc.sync.dma_start(w2_raw[:, 1:PACK, :], w2_rows[:, 1:PACK, :])
+        x_table = keep.tile([P, T], I32, name="x_table", align_bytes=64)
+        nc.sync.dma_start(x_table[:], x_words[0].rearrange("p c r -> p (c r)").bitcast(I32))
 
-        s_picked = keep.tile([P, S], U8, name="s_picked", align_bytes=64)
+        s_picked = keep.tile([P, S], U8, name="s_picked", tag="late", align_bytes=64)
         nc.vector.tensor_copy(s_picked[:], s_table[:].indirect(offsets[:]))
         nc.vector.tensor_copy(planes[:, 0:S].bitcast(I32), s_picked[:].bitcast(I32))
         for i in range(1, 4):
             nc.sync.dma_start(planes[i:P:32, :].bitcast(I32), planes[8 * i : P : 32, :].bitcast(I32))
+
+        w13_codes = keep.tile([P, 2 * N], I32, name="w13_codes", tag="late", align_bytes=64)
+        nc.sync.dma_start(w13_codes[:, 0:N], w1_words[0].rearrange("p c r -> p (c r)").bitcast(I32))
+        nc.sync.dma_start(w13_codes[:, N : 2 * N], w3_words[0].rearrange("p c r -> p (c r)").bitcast(I32))
 
         w2_codes = keep.tile([P, H], U32, name="w2_codes", align_bytes=64)
         w2_plane = keep.tile([P, H], U8, name="w2_plane", align_bytes=64)
@@ -68,6 +72,18 @@ def tile_picked_phlora_none_p_kernel(
                 out=w2_codes[:, u * HALF : (u + 1) * HALF].bitcast(FP8X4),
                 scales=w2_plane[:, u * HALF : (u + 1) * HALF],
                 in_=w2_bf[:],
+            )
+
+        warm_bank = psum.tile([64, PACK, CHUNK], F32, name="warm_bank", tag="acc3")
+        for r in range(12):
+            nc.tensor.matmul_mx(
+                out=warm_bank[:, r % PACK, :],
+                lhsT=w2_codes[:, 0:64].bitcast(FP8X4),
+                lhsT_scale=w2_plane[:, 0:64],
+                rhs=w2_codes[:, P : 2 * P].bitcast(FP8X4),
+                rhs_scale=w2_plane[:, P : 2 * P],
+                start=True,
+                stop=True,
             )
 
         x_picked = keep.tile([P, S], U32, name="x_picked", tag="slot1", align_bytes=64)
@@ -101,10 +117,10 @@ def tile_picked_phlora_none_p_kernel(
         accs = []
         for c in range(chunks):
             codes, plane = x_operand(c)
-            acc = psum.tile([P, CHUNK], F32, name=f"acc{c}")
+            acc = psum.tile([P, CHUNK], F32, name=f"acc{c}", tag=f"acc{c}")
             nc.tensor.matmul_mx(
                 out=acc[:],
-                lhsT=w1_codes[:].bitcast(FP8X4),
+                lhsT=w13_codes[:, 0:N].bitcast(FP8X4),
                 lhsT_scale=planes[:, S : S + N],
                 rhs=codes,
                 rhs_scale=plane,
@@ -122,7 +138,7 @@ def tile_picked_phlora_none_p_kernel(
             nc.vector.quantize_mx(out=h_codes[:].bitcast(FP8X4), scales=h_plane[:], in_=h_bf[:])
             nc.tensor.matmul_mx(
                 out=accs[c][:],
-                lhsT=w3_codes[:].bitcast(FP8X4),
+                lhsT=w13_codes[:, N : 2 * N].bitcast(FP8X4),
                 lhsT_scale=planes[:, S + N : S + 2 * N],
                 rhs=h_codes[:].bitcast(FP8X4),
                 rhs_scale=h_plane[:],

@@ -15,115 +15,128 @@ FP8X4 = mybir.dt.float8_e4m3fn_x4
 
 P = 128
 PACK = 4
+BLOCK_ROWS = 8
+QUADRANT = 32
+LIST_ROWS = 16
 CHUNK = 128
-HALF = 256
+GATHER = 256
+PAIR = 2
+FIRST_ROWS = 1
+WARM_PASSES = 12
+WARM_COLUMNS = 64
 
 
 def tile_picked_phlora_none_p_kernel(
     tc, x_words, x_scales, w1_words, w1_scales, w2, w3_words, w3_scales, offs, out
 ):
     nc = tc.nc
+    chunks = S // CHUNK
     with ExitStack() as ctx:
         keep = ctx.enter_context(tc.tile_pool(name="keep", bufs=1))
         psum = ctx.enter_context(tc.psum_pool(name="psum", bufs=1))
 
         w2_rows = w2.rearrange("(p j) c -> p j c", j=PACK)
-        w2_raw = keep.tile([P, PACK, H], F32, name="w2_raw")
-        nc.sync.dma_start(w2_raw[:, 0:1, :], w2_rows[:, 0:1, :])
+        w2_raw = keep.tile([P, PACK, H], F32, name="w2_raw", tag="w2_raw_then_x_picked", align_bytes=64)
+        nc.sync.dma_start(w2_raw[:, 0:FIRST_ROWS, :], w2_rows[:, 0:FIRST_ROWS, :])
 
-        offsets = keep.tile([P, S // 16], U16, name="offsets")
+        offsets = keep.tile([P, S // LIST_ROWS], U16, name="offsets")
         nc.sync.dma_start(offsets[:], offs)
 
-        s_table = keep.tile([P, T], U8, name="s_table", align_bytes=64)
-        nc.vector.memset(s_table[:].bitcast(I32), 0)
-        nc.sync.dma_start(s_table[0:P:8, :].bitcast(I32), x_scales[0].bitcast(I32))
+        scale_table = keep.tile([P, T], U8, name="scale_table", align_bytes=64)
+        nc.vector.memset(scale_table[:].bitcast(I32), 0)
+        nc.sync.dma_start(scale_table[0:P:BLOCK_ROWS, :].bitcast(I32), x_scales[0].bitcast(I32))
 
         planes = keep.tile([P, S + 2 * N], U8, name="planes", align_bytes=64)
+        w1_plane_cols = slice(S, S + N)
+        w3_plane_cols = slice(S + N, S + 2 * N)
         nc.vector.memset(planes[:, S : S + 2 * N].bitcast(I32), 0)
-        nc.scalar.dma_start(planes[0:P:8, S : S + N].bitcast(I32), w1_scales[0].bitcast(I32))
-        nc.scalar.dma_start(planes[0:P:8, S + N : S + 2 * N].bitcast(I32), w3_scales[0].bitcast(I32))
+        nc.scalar.dma_start(planes[0:P:BLOCK_ROWS, w1_plane_cols].bitcast(I32), w1_scales[0].bitcast(I32))
+        nc.scalar.dma_start(planes[0:P:BLOCK_ROWS, w3_plane_cols].bitcast(I32), w3_scales[0].bitcast(I32))
 
         warm_in = keep.tile([P, 1], F32, name="warm_in")
         warm_out = keep.tile([P, 1], F32, name="warm_out")
         nc.gpsimd.memset(warm_in[:], 0.0)
         nc.scalar.copy(warm_out[:], warm_in[:])
 
-        nc.sync.dma_start(w2_raw[:, 1:PACK, :], w2_rows[:, 1:PACK, :])
-        x_table = keep.tile([P, T], I32, name="x_table", align_bytes=64)
-        nc.sync.dma_start(x_table[:], x_words[0].rearrange("p c r -> p (c r)").bitcast(I32))
+        nc.sync.dma_start(w2_raw[:, FIRST_ROWS:PACK, :], w2_rows[:, FIRST_ROWS:PACK, :])
+        word_table = keep.tile([P, T], I32, name="word_table", align_bytes=64)
+        nc.sync.dma_start(word_table[:], x_words[0].rearrange("p c r -> p (c r)").bitcast(I32))
 
-        s_picked = keep.tile([P, S], U8, name="s_picked", tag="late", align_bytes=64)
-        nc.vector.tensor_copy(s_picked[:], s_table[:].indirect(offsets[:]))
-        nc.vector.tensor_copy(planes[:, 0:S].bitcast(I32), s_picked[:].bitcast(I32))
-        for i in range(1, 4):
-            nc.sync.dma_start(planes[i:P:32, :].bitcast(I32), planes[8 * i : P : 32, :].bitcast(I32))
+        scales_picked = keep.tile([P, S], U8, name="scales_picked", tag="scales_then_w13", align_bytes=64)
+        nc.vector.tensor_copy(scales_picked[:], scale_table[:].indirect(offsets[:]))
+        nc.vector.tensor_copy(planes[:, 0:S].bitcast(I32), scales_picked[:].bitcast(I32))
+        for i in range(1, QUADRANT // BLOCK_ROWS):
+            nc.sync.dma_start(
+                planes[i:P:QUADRANT, :].bitcast(I32), planes[BLOCK_ROWS * i : P : QUADRANT, :].bitcast(I32)
+            )
 
-        w13_codes = keep.tile([P, 2 * N], I32, name="w13_codes", tag="late", align_bytes=64)
+        w13_codes = keep.tile([P, 2 * N], I32, name="w13_codes", tag="scales_then_w13", align_bytes=64)
         nc.sync.dma_start(w13_codes[:, 0:N], w1_words[0].rearrange("p c r -> p (c r)").bitcast(I32))
         nc.sync.dma_start(w13_codes[:, N : 2 * N], w3_words[0].rearrange("p c r -> p (c r)").bitcast(I32))
 
         w2_codes = keep.tile([P, H], U32, name="w2_codes", align_bytes=64)
         w2_plane = keep.tile([P, H], U8, name="w2_plane", align_bytes=64)
         w2_src = w2_raw[:].rearrange("p j (m t) -> p m j t", t=PACK)
-        for u, copy in enumerate((nc.vector.tensor_copy, nc.scalar.copy)):
-            w2_bf = keep.tile([P, 2 * H], BF16, name=f"w2_bf{u}", tag=f"slot{u}", align_bytes=64)
-            copy(w2_bf[:].rearrange("p (t m j) -> p m j t", t=2, j=PACK), w2_src[:, :, :, 2 * u : 2 * u + 2])
+        for u, round_copy in enumerate((nc.vector.tensor_copy, nc.scalar.copy)):
+            w2_bf = keep.tile([P, PAIR * P * PACK], BF16, name=f"w2_bf{u}", align_bytes=64)
+            round_copy(
+                w2_bf[:].rearrange("p (t m j) -> p m j t", t=PAIR, j=PACK),
+                w2_src[:, :, :, PAIR * u : PAIR * (u + 1)],
+            )
+            pair_cols = slice(PAIR * P * u, PAIR * P * (u + 1))
             nc.vector.quantize_mx(
-                out=w2_codes[:, u * HALF : (u + 1) * HALF].bitcast(FP8X4),
-                scales=w2_plane[:, u * HALF : (u + 1) * HALF],
-                in_=w2_bf[:],
+                out=w2_codes[:, pair_cols].bitcast(FP8X4), scales=w2_plane[:, pair_cols], in_=w2_bf[:]
             )
 
-        warm_bank = psum.tile([64, PACK, CHUNK], F32, name="warm_bank", tag="acc3")
-        for r in range(12):
+        warm_bank = psum.tile([WARM_COLUMNS, PACK, CHUNK], F32, name="warm_bank", tag=f"acc{chunks - 1}")
+        for r in range(WARM_PASSES):
             nc.tensor.matmul_mx(
                 out=warm_bank[:, r % PACK, :],
-                lhsT=w2_codes[:, 0:64].bitcast(FP8X4),
-                lhsT_scale=w2_plane[:, 0:64],
-                rhs=w2_codes[:, P : 2 * P].bitcast(FP8X4),
-                rhs_scale=w2_plane[:, P : 2 * P],
+                lhsT=w2_codes[:, 0:WARM_COLUMNS].bitcast(FP8X4),
+                lhsT_scale=w2_plane[:, 0:WARM_COLUMNS],
+                rhs=w2_codes[:, P : P + CHUNK].bitcast(FP8X4),
+                rhs_scale=w2_plane[:, P : P + CHUNK],
                 start=True,
                 stop=True,
             )
 
-        x_picked = keep.tile([P, S], U32, name="x_picked", tag="slot1", align_bytes=64)
-        for a in range(S // HALF):
+        x_picked = keep.tile([P, S], U32, name="x_picked", tag="w2_raw_then_x_picked", align_bytes=64)
+        for a in range(S // GATHER):
             nc.vector.tensor_copy(
-                x_picked[:, a * HALF : (a + 1) * HALF],
-                x_table[:].bitcast(U32).indirect(offsets[:, a * HALF // 16 : (a + 1) * HALF // 16]),
+                x_picked[:, a * GATHER : (a + 1) * GATHER],
+                word_table[:].bitcast(U32).indirect(offsets[:, a * GATHER // LIST_ROWS : (a + 1) * GATHER // LIST_ROWS]),
             )
 
         def x_operand(c):
             cols = slice(c * CHUNK, (c + 1) * CHUNK)
             return x_picked[:, cols].bitcast(FP8X4), planes[:, cols]
 
-        chunks = S // CHUNK
         h_banks = []
         for c in range(chunks):
-            codes, plane = x_operand(c)
-            bank = psum.tile([P, PACK, CHUNK], F32, name=f"h_bank{c}")
+            x_codes, x_plane = x_operand(c)
+            h_bank = psum.tile([P, PACK, CHUNK], F32, name=f"h_bank{c}")
             for t in range(PACK):
                 nc.tensor.matmul_mx(
-                    out=bank[:, t, :],
+                    out=h_bank[:, t, :],
                     lhsT=w2_codes[:, t * P : (t + 1) * P].bitcast(FP8X4),
                     lhsT_scale=w2_plane[:, t * P : (t + 1) * P],
-                    rhs=codes,
-                    rhs_scale=plane,
+                    rhs=x_codes,
+                    rhs_scale=x_plane,
                     start=True,
                     stop=True,
                 )
-            h_banks.append(bank)
+            h_banks.append(h_bank)
 
         accs = []
         for c in range(chunks):
-            codes, plane = x_operand(c)
+            x_codes, x_plane = x_operand(c)
             acc = psum.tile([P, CHUNK], F32, name=f"acc{c}", tag=f"acc{c}")
             nc.tensor.matmul_mx(
                 out=acc[:],
                 lhsT=w13_codes[:, 0:N].bitcast(FP8X4),
-                lhsT_scale=planes[:, S : S + N],
-                rhs=codes,
-                rhs_scale=plane,
+                lhsT_scale=planes[:, w1_plane_cols],
+                rhs=x_codes,
+                rhs_scale=x_plane,
                 start=True,
                 stop=False,
             )
@@ -131,7 +144,7 @@ def tile_picked_phlora_none_p_kernel(
 
         for c in range(chunks):
             h_bf = keep.tile([P, CHUNK * PACK], BF16, name=f"h_bf{c}", align_bytes=64)
-            h_copy = nc.vector.tensor_copy if c == 2 else nc.scalar.copy
+            h_copy = nc.vector.tensor_copy if c == chunks - 2 else nc.scalar.copy
             h_copy(h_bf[:].rearrange("p (n t) -> p n t", t=PACK), h_banks[c][:].rearrange("p t n -> p n t"))
             h_codes = keep.tile([P, CHUNK], U32, name=f"h_codes{c}", align_bytes=64)
             h_plane = keep.tile([P, CHUNK], U8, name=f"h_plane{c}", align_bytes=64)
@@ -139,7 +152,7 @@ def tile_picked_phlora_none_p_kernel(
             nc.tensor.matmul_mx(
                 out=accs[c][:],
                 lhsT=w13_codes[:, N : 2 * N].bitcast(FP8X4),
-                lhsT_scale=planes[:, S + N : S + 2 * N],
+                lhsT_scale=planes[:, w3_plane_cols],
                 rhs=h_codes[:].bitcast(FP8X4),
                 rhs_scale=h_plane[:],
                 start=False,

@@ -22,7 +22,7 @@ CHUNK = 128
 GATHER = 256
 PAIR = 2
 FIRST_ROWS = 1
-WARM_PASSES = 12
+WARM_PASSES = 2
 WARM_COLUMNS = 64
 
 
@@ -53,11 +53,6 @@ def tile_picked_phlora_none_p_kernel(
         nc.scalar.dma_start(planes[0:P:BLOCK_ROWS, w1_plane_cols].bitcast(I32), w1_scales[0].bitcast(I32))
         nc.scalar.dma_start(planes[0:P:BLOCK_ROWS, w3_plane_cols].bitcast(I32), w3_scales[0].bitcast(I32))
 
-        warm_in = keep.tile([P, 1], F32, name="warm_in")
-        warm_out = keep.tile([P, 1], F32, name="warm_out")
-        nc.gpsimd.memset(warm_in[:], 0.0)
-        nc.scalar.copy(warm_out[:], warm_in[:])
-
         nc.sync.dma_start(w2_raw[:, FIRST_ROWS:PACK, :], w2_rows[:, FIRST_ROWS:PACK, :])
         word_table = keep.tile([P, T], I32, name="word_table", align_bytes=64)
         nc.sync.dma_start(word_table[:], x_words[0].rearrange("p c r -> p (c r)").bitcast(I32))
@@ -77,25 +72,25 @@ def tile_picked_phlora_none_p_kernel(
         w2_codes = keep.tile([P, H], U32, name="w2_codes", align_bytes=64)
         w2_plane = keep.tile([P, H], U8, name="w2_plane", align_bytes=64)
         w2_src = w2_raw[:].rearrange("p j (m t) -> p m j t", t=PACK)
+        row_pieces = ((slice(0, PACK),), (slice(0, FIRST_ROWS), slice(FIRST_ROWS, PACK)))
         for u, round_copy in enumerate((nc.vector.tensor_copy, nc.scalar.copy)):
             w2_bf = keep.tile([P, PAIR * P * PACK], BF16, name=f"w2_bf{u}", align_bytes=64)
-            round_copy(
-                w2_bf[:].rearrange("p (t m j) -> p m j t", t=PAIR, j=PACK),
-                w2_src[:, :, :, PAIR * u : PAIR * (u + 1)],
-            )
+            w2_dst = w2_bf[:].rearrange("p (t m j) -> p m j t", t=PAIR, j=PACK)
+            for rows in row_pieces[u]:
+                round_copy(w2_dst[:, :, rows, :], w2_src[:, :, rows, PAIR * u : PAIR * (u + 1)])
             pair_cols = slice(PAIR * P * u, PAIR * P * (u + 1))
             nc.vector.quantize_mx(
                 out=w2_codes[:, pair_cols].bitcast(FP8X4), scales=w2_plane[:, pair_cols], in_=w2_bf[:]
             )
 
-        warm_bank = psum.tile([WARM_COLUMNS, PACK, CHUNK], F32, name="warm_bank", tag=f"acc{chunks - 1}")
+        warm_bank = psum.tile([WARM_COLUMNS, H], F32, name="warm_bank", tag=f"acc{chunks - 1}")
         for r in range(WARM_PASSES):
             nc.tensor.matmul_mx(
-                out=warm_bank[:, r % PACK, :],
+                out=warm_bank[:],
                 lhsT=w2_codes[:, 0:WARM_COLUMNS].bitcast(FP8X4),
                 lhsT_scale=w2_plane[:, 0:WARM_COLUMNS],
-                rhs=w2_codes[:, P : P + CHUNK].bitcast(FP8X4),
-                rhs_scale=w2_plane[:, P : P + CHUNK],
+                rhs=w2_codes[:].bitcast(FP8X4),
+                rhs_scale=w2_plane[:],
                 start=True,
                 stop=True,
             )
@@ -145,10 +140,19 @@ def tile_picked_phlora_none_p_kernel(
         for c in range(chunks):
             h_bf = keep.tile([P, CHUNK * PACK], BF16, name=f"h_bf{c}", align_bytes=64)
             h_copy = nc.vector.tensor_copy if c == chunks - 2 else nc.scalar.copy
-            h_copy(h_bf[:].rearrange("p (n t) -> p n t", t=PACK), h_banks[c][:].rearrange("p t n -> p n t"))
             h_codes = keep.tile([P, CHUNK], U32, name=f"h_codes{c}", align_bytes=64)
             h_plane = keep.tile([P, CHUNK], U8, name=f"h_plane{c}", align_bytes=64)
-            nc.vector.quantize_mx(out=h_codes[:].bitcast(FP8X4), scales=h_plane[:], in_=h_bf[:])
+            width = CHUNK // 2 if c == chunks - 1 else CHUNK
+            for n0 in range(0, CHUNK, width):
+                places = slice(n0, n0 + width)
+                values = slice(PACK * n0, PACK * (n0 + width))
+                h_copy(
+                    h_bf[:, values].rearrange("p (n t) -> p n t", t=PACK),
+                    h_banks[c][:, :, places].rearrange("p t n -> p n t"),
+                )
+                nc.vector.quantize_mx(
+                    out=h_codes[:, places].bitcast(FP8X4), scales=h_plane[:, places], in_=h_bf[:, values]
+                )
             nc.tensor.matmul_mx(
                 out=accs[c][:],
                 lhsT=w13_codes[:, N : 2 * N].bitcast(FP8X4),

@@ -24,6 +24,8 @@ PAIR = 2
 FIRST_ROWS = 1
 WARM_PASSES = 2
 WARM_COLUMNS = 64
+WARM_WIDTH = 512
+PAD = WARM_WIDTH - PAIR * P
 
 
 def tile_picked_phlora_none_p_kernel(
@@ -46,12 +48,13 @@ def tile_picked_phlora_none_p_kernel(
         nc.vector.memset(scale_table[:].bitcast(I32), 0)
         nc.sync.dma_start(scale_table[0:P:BLOCK_ROWS, :].bitcast(I32), x_scales[0].bitcast(I32))
 
+        staged = keep.tile([P, S + 2 * N], U8, name="staged", align_bytes=64)
         planes = keep.tile([P, S + 2 * N], U8, name="planes", align_bytes=64)
         w1_plane_cols = slice(S, S + N)
         w3_plane_cols = slice(S + N, S + 2 * N)
-        nc.vector.memset(planes[:, S : S + 2 * N].bitcast(I32), 0)
-        nc.scalar.dma_start(planes[0:P:BLOCK_ROWS, w1_plane_cols].bitcast(I32), w1_scales[0].bitcast(I32))
-        nc.scalar.dma_start(planes[0:P:BLOCK_ROWS, w3_plane_cols].bitcast(I32), w3_scales[0].bitcast(I32))
+        nc.scalar.dma_start(staged[0:P:BLOCK_ROWS, w1_plane_cols].bitcast(I32), w1_scales[0].bitcast(I32))
+        nc.scalar.dma_start(staged[0:P:BLOCK_ROWS, w3_plane_cols].bitcast(I32), w3_scales[0].bitcast(I32))
+        nc.vector.memset(planes[:].bitcast(I32), 0)
 
         nc.sync.dma_start(w2_raw[:, FIRST_ROWS:PACK, :], w2_rows[:, FIRST_ROWS:PACK, :])
         word_table = keep.tile([P, T], I32, name="word_table", align_bytes=64)
@@ -59,38 +62,55 @@ def tile_picked_phlora_none_p_kernel(
 
         scales_picked = keep.tile([P, S], U8, name="scales_picked", tag="scales_then_w13", align_bytes=64)
         nc.vector.tensor_copy(scales_picked[:], scale_table[:].indirect(offsets[:]))
-        nc.vector.tensor_copy(planes[:, 0:S].bitcast(I32), scales_picked[:].bitcast(I32))
-        for i in range(1, QUADRANT // BLOCK_ROWS):
+        nc.vector.tensor_copy(staged[:, 0:S].bitcast(I32), scales_picked[:].bitcast(I32))
+        for i in range(QUADRANT // BLOCK_ROWS):
             nc.sync.dma_start(
-                planes[i:P:QUADRANT, :].bitcast(I32), planes[BLOCK_ROWS * i : P : QUADRANT, :].bitcast(I32)
+                planes[i:P:QUADRANT, :].bitcast(I32), staged[BLOCK_ROWS * i : P : QUADRANT, :].bitcast(I32)
             )
 
         w13_codes = keep.tile([P, 2 * N], I32, name="w13_codes", tag="scales_then_w13", align_bytes=64)
         nc.sync.dma_start(w13_codes[:, 0:N], w1_words[0].rearrange("p c r -> p (c r)").bitcast(I32))
         nc.sync.dma_start(w13_codes[:, N : 2 * N], w3_words[0].rearrange("p c r -> p (c r)").bitcast(I32))
 
-        w2_codes = keep.tile([P, H], U32, name="w2_codes", align_bytes=64)
-        w2_plane = keep.tile([P, H], U8, name="w2_plane", align_bytes=64)
+        padded_codes = keep.tile([P, PAD + H], I32, name="padded_codes", align_bytes=64)
+        padded_plane = keep.tile([P, PAD + H], U8, name="padded_plane", align_bytes=64)
+        nc.vector.memset(padded_codes[:, 0:PAD], 0)
+        nc.vector.memset(padded_plane[:, 0:PAD].bitcast(I32), 0)
         w2_src = w2_raw[:].rearrange("p j (m t) -> p m j t", t=PACK)
-        row_pieces = ((slice(0, PACK),), (slice(0, FIRST_ROWS), slice(FIRST_ROWS, PACK)))
-        for u, round_copy in enumerate((nc.vector.tensor_copy, nc.scalar.copy)):
-            w2_bf = keep.tile([P, PAIR * P * PACK], BF16, name=f"w2_bf{u}", align_bytes=64)
-            w2_dst = w2_bf[:].rearrange("p (t m j) -> p m j t", t=PAIR, j=PACK)
-            for rows in row_pieces[u]:
-                round_copy(w2_dst[:, :, rows, :], w2_src[:, :, rows, PAIR * u : PAIR * (u + 1)])
-            pair_cols = slice(PAIR * P * u, PAIR * P * (u + 1))
-            nc.vector.quantize_mx(
-                out=w2_codes[:, pair_cols].bitcast(FP8X4), scales=w2_plane[:, pair_cols], in_=w2_bf[:]
-            )
 
-        warm_bank = psum.tile([WARM_COLUMNS, H], F32, name="warm_bank", tag=f"acc{chunks - 1}")
+        def w2_operand(first, count):
+            cols = slice(PAD + first, PAD + first + count)
+            return padded_codes[:, cols].bitcast(FP8X4), padded_plane[:, cols]
+
+        def quantise_w2(rounded, first, count):
+            codes, plane = w2_operand(first, count)
+            start = PACK * (first % (PAIR * P))
+            nc.vector.quantize_mx(out=codes, scales=plane, in_=rounded[:, start : start + PACK * count])
+
+        vector_pair = keep.tile([P, PAIR * P * PACK], BF16, name="vector_pair", align_bytes=64)
+        vector_dst = vector_pair[:].rearrange("p (t m j) -> p m j t", t=PAIR, j=PACK)
+        halves = (slice(0, P // 2), slice(P // 2, P))
+        for m_half in halves:
+            nc.vector.tensor_copy(vector_dst[:, m_half, :, :], w2_src[:, m_half, :, 0:PAIR])
+        for m_half in halves:
+            for t in range(PAIR):
+                quantise_w2(vector_pair, P * t + m_half.start, P // 2)
+
+        scalar_pair = keep.tile([P, PAIR * P * PACK], BF16, name="scalar_pair", align_bytes=64)
+        scalar_dst = scalar_pair[:].rearrange("p (t m j) -> p m j t", t=PAIR, j=PACK)
+        for rows in (slice(0, FIRST_ROWS), slice(FIRST_ROWS, PACK)):
+            nc.scalar.copy(scalar_dst[:, :, rows, :], w2_src[:, :, rows, PAIR:PACK])
+        quantise_w2(scalar_pair, PAIR * P, PAIR * P)
+
+        warm_bank = psum.tile([WARM_COLUMNS, WARM_WIDTH], F32, name="warm_bank", tag=f"acc{chunks - 1}")
+        first_codes, first_plane = w2_operand(0, WARM_COLUMNS)
         for r in range(WARM_PASSES):
             nc.tensor.matmul_mx(
                 out=warm_bank[:],
-                lhsT=w2_codes[:, 0:WARM_COLUMNS].bitcast(FP8X4),
-                lhsT_scale=w2_plane[:, 0:WARM_COLUMNS],
-                rhs=w2_codes[:].bitcast(FP8X4),
-                rhs_scale=w2_plane[:],
+                lhsT=first_codes,
+                lhsT_scale=first_plane,
+                rhs=padded_codes[:, 0:WARM_WIDTH].bitcast(FP8X4),
+                rhs_scale=padded_plane[:, 0:WARM_WIDTH],
                 start=True,
                 stop=True,
             )
@@ -111,10 +131,11 @@ def tile_picked_phlora_none_p_kernel(
             x_codes, x_plane = x_operand(c)
             h_bank = psum.tile([P, PACK, CHUNK], F32, name=f"h_bank{c}")
             for t in range(PACK):
+                w2_codes, w2_plane = w2_operand(t * P, P)
                 nc.tensor.matmul_mx(
                     out=h_bank[:, t, :],
-                    lhsT=w2_codes[:, t * P : (t + 1) * P].bitcast(FP8X4),
-                    lhsT_scale=w2_plane[:, t * P : (t + 1) * P],
+                    lhsT=w2_codes,
+                    lhsT_scale=w2_plane,
                     rhs=x_codes,
                     rhs_scale=x_plane,
                     start=True,
@@ -163,8 +184,10 @@ def tile_picked_phlora_none_p_kernel(
                 stop=True,
             )
 
+        result = keep.tile([P, S], F32, name="result")
         for c in range(chunks):
-            result = keep.tile([P, CHUNK], F32, name=f"result{c}")
             out_copy = nc.vector.tensor_copy if c == chunks - 1 else nc.scalar.copy
-            out_copy(result[:], accs[c][:])
-            nc.sync.dma_start(out[:, c * CHUNK : (c + 1) * CHUNK], result[:])
+            out_copy(result[:, c * CHUNK : (c + 1) * CHUNK], accs[c][:])
+            if c > 0:
+                first = 0 if c == 1 else c * CHUNK
+                nc.sync.dma_start(out[:, first : (c + 1) * CHUNK], result[:, first : (c + 1) * CHUNK])

@@ -21,11 +21,12 @@ LIST_ROWS = 16
 CHUNK = 128
 GATHER = 256
 PAIR = 2
-FIRST_ROWS = 1
+FIRST_PIECE = 768
+FIRST_ROWS = FIRST_PIECE // H
 WARM_PASSES = 2
 WARM_COLUMNS = 64
 WARM_WIDTH = 512
-PAD = WARM_WIDTH - PAIR * P
+PAD = WARM_WIDTH - WARM_COLUMNS
 
 
 def tile_picked_phlora_none_p_kernel(
@@ -37,9 +38,9 @@ def tile_picked_phlora_none_p_kernel(
         keep = ctx.enter_context(tc.tile_pool(name="keep", bufs=1))
         psum = ctx.enter_context(tc.psum_pool(name="psum", bufs=1))
 
-        w2_rows = w2.rearrange("(p j) c -> p j c", j=PACK)
-        w2_raw = keep.tile([P, PACK, H], F32, name="w2_raw", tag="w2_raw_then_x_picked", align_bytes=64)
-        nc.sync.dma_start(w2_raw[:, 0:FIRST_ROWS, :], w2_rows[:, 0:FIRST_ROWS, :])
+        w2_rows = w2.rearrange("(p j) c -> p (j c)", j=PACK)
+        w2_raw = keep.tile([P, PACK * H], F32, name="w2_raw", tag="w2_raw_then_x_picked", align_bytes=64)
+        nc.sync.dma_start(w2_raw[:, 0:FIRST_PIECE], w2_rows[:, 0:FIRST_PIECE])
 
         offsets = keep.tile([P, S // LIST_ROWS], U16, name="offsets")
         nc.sync.dma_start(offsets[:], offs)
@@ -56,7 +57,7 @@ def tile_picked_phlora_none_p_kernel(
         nc.scalar.dma_start(staged[0:P:BLOCK_ROWS, w3_plane_cols].bitcast(I32), w3_scales[0].bitcast(I32))
         nc.vector.memset(planes[:].bitcast(I32), 0)
 
-        nc.sync.dma_start(w2_raw[:, FIRST_ROWS:PACK, :], w2_rows[:, FIRST_ROWS:PACK, :])
+        nc.sync.dma_start(w2_raw[:, FIRST_PIECE : PACK * H], w2_rows[:, FIRST_PIECE : PACK * H])
         word_table = keep.tile([P, T], I32, name="word_table", align_bytes=64)
         nc.sync.dma_start(word_table[:], x_words[0].rearrange("p c r -> p (c r)").bitcast(I32))
 
@@ -76,7 +77,7 @@ def tile_picked_phlora_none_p_kernel(
         padded_plane = keep.tile([P, PAD + H], U8, name="padded_plane", align_bytes=64)
         nc.vector.memset(padded_codes[:, 0:PAD], 0)
         nc.vector.memset(padded_plane[:, 0:PAD].bitcast(I32), 0)
-        w2_src = w2_raw[:].rearrange("p j (m t) -> p m j t", t=PACK)
+        w2_src = w2_raw[:].rearrange("p (j m t) -> p m j t", j=PACK, t=PACK)
 
         def w2_operand(first, count):
             cols = slice(PAD + first, PAD + first + count)
@@ -103,7 +104,7 @@ def tile_picked_phlora_none_p_kernel(
         quantise_w2(scalar_pair, PAIR * P, PAIR * P)
 
         warm_bank = psum.tile([WARM_COLUMNS, WARM_WIDTH], F32, name="warm_bank", tag=f"acc{chunks - 1}")
-        first_codes, first_plane = w2_operand(0, WARM_COLUMNS)
+        first_codes, first_plane = w2_operand(P, WARM_COLUMNS)
         for r in range(WARM_PASSES):
             nc.tensor.matmul_mx(
                 out=warm_bank[:],

@@ -26,7 +26,7 @@ FIRST_ROWS = FIRST_PIECE // H
 WARM_PASSES = 2
 WARM_COLUMNS = 64
 WARM_WIDTH = 512
-PAD = WARM_WIDTH - WARM_COLUMNS
+PAD = WARM_WIDTH - P
 
 
 def tile_picked_phlora_none_p_kernel(
@@ -38,7 +38,7 @@ def tile_picked_phlora_none_p_kernel(
         keep = ctx.enter_context(tc.tile_pool(name="keep", bufs=1))
         psum = ctx.enter_context(tc.psum_pool(name="psum", bufs=1))
 
-        w2_rows = w2.rearrange("(p j) c -> p (j c)", j=PACK)
+        w2_rows = w2.rearrange("(p j) col -> p (j col)", j=PACK)
         w2_raw = keep.tile([P, PACK * H], F32, name="w2_raw", tag="w2_raw_then_x_picked", align_bytes=64)
         nc.sync.dma_start(w2_raw[:, 0:FIRST_PIECE], w2_rows[:, 0:FIRST_PIECE])
 
@@ -59,19 +59,19 @@ def tile_picked_phlora_none_p_kernel(
 
         nc.sync.dma_start(w2_raw[:, FIRST_PIECE : PACK * H], w2_rows[:, FIRST_PIECE : PACK * H])
         word_table = keep.tile([P, T], I32, name="word_table", align_bytes=64)
-        nc.sync.dma_start(word_table[:], x_words[0].rearrange("p c r -> p (c r)").bitcast(I32))
+        nc.sync.dma_start(word_table[:], x_words[0].rearrange("p col byte -> p (col byte)").bitcast(I32))
 
         scales_picked = keep.tile([P, S], U8, name="scales_picked", tag="scales_then_w13", align_bytes=64)
         nc.vector.tensor_copy(scales_picked[:], scale_table[:].indirect(offsets[:]))
         nc.vector.tensor_copy(staged[:, 0:S].bitcast(I32), scales_picked[:].bitcast(I32))
-        for i in range(QUADRANT // BLOCK_ROWS):
+        for e in range(QUADRANT // BLOCK_ROWS):
             nc.sync.dma_start(
-                planes[i:P:QUADRANT, :].bitcast(I32), staged[BLOCK_ROWS * i : P : QUADRANT, :].bitcast(I32)
+                planes[e:P:QUADRANT, :].bitcast(I32), staged[BLOCK_ROWS * e : P : QUADRANT, :].bitcast(I32)
             )
 
         w13_codes = keep.tile([P, 2 * N], I32, name="w13_codes", tag="scales_then_w13", align_bytes=64)
-        nc.sync.dma_start(w13_codes[:, 0:N], w1_words[0].rearrange("p c r -> p (c r)").bitcast(I32))
-        nc.sync.dma_start(w13_codes[:, N : 2 * N], w3_words[0].rearrange("p c r -> p (c r)").bitcast(I32))
+        nc.sync.dma_start(w13_codes[:, 0:N], w1_words[0].rearrange("p col byte -> p (col byte)").bitcast(I32))
+        nc.sync.dma_start(w13_codes[:, N : 2 * N], w3_words[0].rearrange("p col byte -> p (col byte)").bitcast(I32))
 
         padded_codes = keep.tile([P, PAD + H], I32, name="padded_codes", align_bytes=64)
         padded_plane = keep.tile([P, PAD + H], U8, name="padded_plane", align_bytes=64)
@@ -104,12 +104,12 @@ def tile_picked_phlora_none_p_kernel(
         quantise_w2(scalar_pair, PAIR * P, PAIR * P)
 
         warm_bank = psum.tile([WARM_COLUMNS, WARM_WIDTH], F32, name="warm_bank", tag=f"acc{chunks - 1}")
-        first_codes, first_plane = w2_operand(P, WARM_COLUMNS)
-        for r in range(WARM_PASSES):
+        warm_codes, warm_plane = w2_operand(0, WARM_COLUMNS)
+        for warm_pass in range(WARM_PASSES):
             nc.tensor.matmul_mx(
                 out=warm_bank[:],
-                lhsT=first_codes,
-                lhsT_scale=first_plane,
+                lhsT=warm_codes,
+                lhsT_scale=warm_plane,
                 rhs=padded_codes[:, 0:WARM_WIDTH].bitcast(FP8X4),
                 rhs_scale=padded_plane[:, 0:WARM_WIDTH],
                 start=True,
@@ -186,9 +186,10 @@ def tile_picked_phlora_none_p_kernel(
             )
 
         result = keep.tile([P, S], F32, name="result")
+        store_from = {1: 0, 2: 2 * CHUNK, 3: 3 * CHUNK}
         for c in range(chunks):
             out_copy = nc.vector.tensor_copy if c == chunks - 1 else nc.scalar.copy
             out_copy(result[:, c * CHUNK : (c + 1) * CHUNK], accs[c][:])
-            if c > 0:
-                first = 0 if c == 1 else c * CHUNK
-                nc.sync.dma_start(out[:, first : (c + 1) * CHUNK], result[:, first : (c + 1) * CHUNK])
+            if c in store_from:
+                stored = slice(store_from[c], (c + 1) * CHUNK)
+                nc.sync.dma_start(out[:, stored], result[:, stored])

@@ -21,12 +21,10 @@ LIST_ROWS = 16
 CHUNK = 128
 GATHER = 256
 PAIR = 2
-FIRST_PIECE = 768
-FIRST_ROWS = FIRST_PIECE // H
+HALF_H = H // 2
 WARM_PASSES = 2
 WARM_COLUMNS = 64
 WARM_WIDTH = 512
-PAD = WARM_WIDTH - P
 
 
 def tile_picked_phlora_none_p_kernel(
@@ -38,9 +36,9 @@ def tile_picked_phlora_none_p_kernel(
         keep = ctx.enter_context(tc.tile_pool(name="keep", bufs=1))
         psum = ctx.enter_context(tc.psum_pool(name="psum", bufs=1))
 
-        w2_rows = w2.rearrange("(p j) col -> p (j col)", j=PACK)
-        w2_raw = keep.tile([P, PACK * H], F32, name="w2_raw", tag="w2_raw_then_x_picked", align_bytes=64)
-        nc.sync.dma_start(w2_raw[:, 0:FIRST_PIECE], w2_rows[:, 0:FIRST_PIECE])
+        w2_rows = w2.rearrange("(p j) col -> p j col", j=PACK)
+        early_raw = keep.tile([P, PACK, HALF_H], F32, name="early_raw", align_bytes=64)
+        nc.sync.dma_start(early_raw[:], w2_rows[:, :, 0:HALF_H])
 
         offsets = keep.tile([P, S // LIST_ROWS], U16, name="offsets")
         nc.sync.dma_start(offsets[:], offs)
@@ -49,88 +47,93 @@ def tile_picked_phlora_none_p_kernel(
         nc.vector.memset(scale_table[:].bitcast(I32), 0)
         nc.sync.dma_start(scale_table[0:P:BLOCK_ROWS, :].bitcast(I32), x_scales[0].bitcast(I32))
 
-        staged = keep.tile([P, S + 2 * N], U8, name="staged", align_bytes=64)
         planes = keep.tile([P, S + 2 * N], U8, name="planes", align_bytes=64)
         w1_plane_cols = slice(S, S + N)
         w3_plane_cols = slice(S + N, S + 2 * N)
-        nc.scalar.dma_start(staged[0:P:BLOCK_ROWS, w1_plane_cols].bitcast(I32), w1_scales[0].bitcast(I32))
-        nc.scalar.dma_start(staged[0:P:BLOCK_ROWS, w3_plane_cols].bitcast(I32), w3_scales[0].bitcast(I32))
-        nc.vector.memset(planes[:].bitcast(I32), 0)
+        nc.vector.memset(planes[:, S : S + 2 * N].bitcast(I32), 0)
+        nc.scalar.dma_start(planes[0:P:BLOCK_ROWS, w1_plane_cols].bitcast(I32), w1_scales[0].bitcast(I32))
+        nc.scalar.dma_start(planes[0:P:BLOCK_ROWS, w3_plane_cols].bitcast(I32), w3_scales[0].bitcast(I32))
 
-        nc.sync.dma_start(w2_raw[:, FIRST_PIECE : PACK * H], w2_rows[:, FIRST_PIECE : PACK * H])
+        late_raw = keep.tile([P, PACK, HALF_H], F32, name="late_raw", tag="late_raw_then_x_picked", align_bytes=64)
+        nc.sync.dma_start(late_raw[:], w2_rows[:, :, HALF_H:H])
         word_table = keep.tile([P, T], I32, name="word_table", align_bytes=64)
         nc.sync.dma_start(word_table[:], x_words[0].rearrange("p col byte -> p (col byte)").bitcast(I32))
 
         scales_picked = keep.tile([P, S], U8, name="scales_picked", tag="scales_then_w13", align_bytes=64)
         nc.vector.tensor_copy(scales_picked[:], scale_table[:].indirect(offsets[:]))
-        nc.vector.tensor_copy(staged[:, 0:S].bitcast(I32), scales_picked[:].bitcast(I32))
-        for e in range(QUADRANT // BLOCK_ROWS):
+        nc.vector.tensor_copy(planes[:, 0:S].bitcast(I32), scales_picked[:].bitcast(I32))
+        for e in range(1, QUADRANT // BLOCK_ROWS):
             nc.sync.dma_start(
-                planes[e:P:QUADRANT, :].bitcast(I32), staged[BLOCK_ROWS * e : P : QUADRANT, :].bitcast(I32)
+                planes[e:P:QUADRANT, :].bitcast(I32), planes[BLOCK_ROWS * e : P : QUADRANT, :].bitcast(I32)
             )
 
         w13_codes = keep.tile([P, 2 * N], I32, name="w13_codes", tag="scales_then_w13", align_bytes=64)
         nc.sync.dma_start(w13_codes[:, 0:N], w1_words[0].rearrange("p col byte -> p (col byte)").bitcast(I32))
         nc.sync.dma_start(w13_codes[:, N : 2 * N], w3_words[0].rearrange("p col byte -> p (col byte)").bitcast(I32))
 
-        padded_codes = keep.tile([P, PAD + H], I32, name="padded_codes", align_bytes=64)
-        padded_plane = keep.tile([P, PAD + H], U8, name="padded_plane", align_bytes=64)
-        nc.vector.memset(padded_codes[:, 0:PAD], 0)
-        nc.vector.memset(padded_plane[:, 0:PAD].bitcast(I32), 0)
-        w2_src = w2_raw[:].rearrange("p (j m t) -> p m j t", j=PACK, t=PACK)
+        w2_codes_tile = keep.tile([P, H], U32, name="w2_codes", align_bytes=64)
+        w2_plane_tile = keep.tile([P, H], U8, name="w2_plane", align_bytes=64)
+        half_m = P // 2
 
         def w2_operand(first, count):
-            cols = slice(PAD + first, PAD + first + count)
-            return padded_codes[:, cols].bitcast(FP8X4), padded_plane[:, cols]
+            cols = slice(first, first + count)
+            return w2_codes_tile[:, cols].bitcast(FP8X4), w2_plane_tile[:, cols]
 
-        def quantise_w2(rounded, first, count):
-            codes, plane = w2_operand(first, count)
-            start = PACK * (first % (PAIR * P))
-            nc.vector.quantize_mx(out=codes, scales=plane, in_=rounded[:, start : start + PACK * count])
+        def round_half(copy, raw, rounded, slots):
+            copy(
+                rounded[:].rearrange("p (t m j) -> p m j t", t=PACK, j=PACK)[:, :, :, slots],
+                raw[:].rearrange("p j (m t) -> p m j t", t=PACK)[:, :, :, slots],
+            )
 
-        vector_pair = keep.tile([P, PAIR * P * PACK], BF16, name="vector_pair", align_bytes=64)
-        vector_dst = vector_pair[:].rearrange("p (t m j) -> p m j t", t=PAIR, j=PACK)
-        halves = (slice(0, P // 2), slice(P // 2, P))
-        for m_half in halves:
-            nc.vector.tensor_copy(vector_dst[:, m_half, :, :], w2_src[:, m_half, :, 0:PAIR])
-        for m_half in halves:
-            for t in range(PAIR):
-                quantise_w2(vector_pair, P * t + m_half.start, P // 2)
+        def quantise_half(rounded, first_m):
+            for t in range(PACK):
+                codes, plane = w2_operand(P * t + first_m, half_m)
+                values = slice(t * half_m * PACK, (t + 1) * half_m * PACK)
+                nc.vector.quantize_mx(out=codes, scales=plane, in_=rounded[:, values])
 
-        scalar_pair = keep.tile([P, PAIR * P * PACK], BF16, name="scalar_pair", align_bytes=64)
-        scalar_dst = scalar_pair[:].rearrange("p (t m j) -> p m j t", t=PAIR, j=PACK)
-        for rows in (slice(0, FIRST_ROWS), slice(FIRST_ROWS, PACK)):
-            nc.scalar.copy(scalar_dst[:, :, rows, :], w2_src[:, :, rows, PAIR:PACK])
-        quantise_w2(scalar_pair, PAIR * P, PAIR * P)
+        early_bf = keep.tile([P, PACK * HALF_H], BF16, name="early_bf", align_bytes=64)
+        round_half(nc.scalar.copy, early_raw, early_bf, slice(0, PACK))
 
-        warm_bank = psum.tile([WARM_COLUMNS, WARM_WIDTH], F32, name="warm_bank", tag=f"acc{chunks - 1}")
-        warm_codes, warm_plane = w2_operand(0, WARM_COLUMNS)
+        warm_codes = keep.tile([P, WARM_WIDTH], U32, name="warm_codes", align_bytes=64)
+        warm_plane = keep.tile([P, WARM_WIDTH], U8, name="warm_plane", align_bytes=64)
+        for first in range(0, WARM_WIDTH, HALF_H):
+            cols = slice(first, first + HALF_H)
+            nc.vector.quantize_mx(out=warm_codes[:, cols].bitcast(FP8X4), scales=warm_plane[:, cols], in_=early_bf[:])
+        warm_bank = psum.tile([WARM_COLUMNS, WARM_WIDTH], F32, name="warm_bank", tag=f"acc{chunks - 2}")
         for warm_pass in range(WARM_PASSES):
             nc.tensor.matmul_mx(
                 out=warm_bank[:],
-                lhsT=warm_codes,
-                lhsT_scale=warm_plane,
-                rhs=padded_codes[:, 0:WARM_WIDTH].bitcast(FP8X4),
-                rhs_scale=padded_plane[:, 0:WARM_WIDTH],
+                lhsT=warm_codes[:, 0:WARM_COLUMNS].bitcast(FP8X4),
+                lhsT_scale=warm_plane[:, 0:WARM_COLUMNS],
+                rhs=warm_codes[:].bitcast(FP8X4),
+                rhs_scale=warm_plane[:],
                 start=True,
                 stop=True,
             )
+        quantise_half(early_bf, 0)
 
-        x_picked = keep.tile([P, S], U32, name="x_picked", tag="w2_raw_then_x_picked", align_bytes=64)
+        late_bf = keep.tile([P, PACK * HALF_H], BF16, name="late_bf", align_bytes=64)
+        round_half(nc.scalar.copy, late_raw, late_bf, slice(0, PAIR))
+        round_half(nc.scalar.copy, late_raw, late_bf, slice(PAIR, PACK))
+        quantise_half(late_bf, half_m)
+
+        x_picked = keep.tile([P, S], U32, name="x_picked", tag="late_raw_then_x_picked", align_bytes=64)
         for a in range(S // GATHER):
             nc.vector.tensor_copy(
                 x_picked[:, a * GATHER : (a + 1) * GATHER],
                 word_table[:].bitcast(U32).indirect(offsets[:, a * GATHER // LIST_ROWS : (a + 1) * GATHER // LIST_ROWS]),
             )
 
-        def x_operand(c):
-            cols = slice(c * CHUNK, (c + 1) * CHUNK)
+        def x_operand(first, count):
+            cols = slice(first, first + count)
             return x_picked[:, cols].bitcast(FP8X4), planes[:, cols]
 
+        half = CHUNK // 2
+        pieces = [(c * CHUNK, CHUNK) for c in range(chunks - 1)] + [(S - CHUNK, half), (S - half, half)]
         h_banks = []
-        for c in range(chunks):
-            x_codes, x_plane = x_operand(c)
-            h_bank = psum.tile([P, PACK, CHUNK], F32, name=f"h_bank{c}")
+        for index, (first, count) in enumerate(pieces):
+            x_codes, x_plane = x_operand(first, count)
+            h_bank = psum.tile([P, PACK, count], F32, name=f"h_bank{index}", tag=f"h_bank{index}")
             for t in range(PACK):
                 w2_codes, w2_plane = w2_operand(t * P, P)
                 nc.tensor.matmul_mx(
@@ -144,10 +147,26 @@ def tile_picked_phlora_none_p_kernel(
                 )
             h_banks.append(h_bank)
 
+        h_codes = [keep.tile([P, CHUNK], U32, name=f"h_codes{c}", align_bytes=64) for c in range(chunks)]
+        h_planes = [keep.tile([P, CHUNK], U8, name=f"h_plane{c}", align_bytes=64) for c in range(chunks)]
+        h_bfs = []
+        for index, (first, count) in enumerate(pieces):
+            h_bf = keep.tile([P, count * PACK], BF16, name=f"h_bf{index}", align_bytes=64)
+            h_copy = nc.vector.tensor_copy if index % 2 else nc.scalar.copy
+            h_copy(h_bf[:].rearrange("p (n t) -> p n t", t=PACK), h_banks[index][:].rearrange("p t n -> p n t"))
+            h_bfs.append(h_bf)
+        for index, (first, count) in enumerate(pieces):
+            places = slice(first % CHUNK, first % CHUNK + count)
+            nc.vector.quantize_mx(
+                out=h_codes[first // CHUNK][:, places].bitcast(FP8X4),
+                scales=h_planes[first // CHUNK][:, places],
+                in_=h_bfs[index][:],
+            )
+
         accs = []
         for c in range(chunks):
-            x_codes, x_plane = x_operand(c)
-            acc = psum.tile([P, CHUNK], F32, name=f"acc{c}", tag=f"acc{c}")
+            x_codes, x_plane = x_operand(c * CHUNK, CHUNK)
+            acc = psum.tile([P, CHUNK], F32, name=f"acc{c}", tag="h_bank0" if c == chunks - 1 else f"acc{c}")
             nc.tensor.matmul_mx(
                 out=acc[:],
                 lhsT=w13_codes[:, 0:N].bitcast(FP8X4),
@@ -158,29 +177,13 @@ def tile_picked_phlora_none_p_kernel(
                 stop=False,
             )
             accs.append(acc)
-
         for c in range(chunks):
-            h_bf = keep.tile([P, CHUNK * PACK], BF16, name=f"h_bf{c}", align_bytes=64)
-            h_copy = nc.vector.tensor_copy if c == chunks - 2 else nc.scalar.copy
-            h_codes = keep.tile([P, CHUNK], U32, name=f"h_codes{c}", align_bytes=64)
-            h_plane = keep.tile([P, CHUNK], U8, name=f"h_plane{c}", align_bytes=64)
-            width = CHUNK // 2 if c == chunks - 1 else CHUNK
-            for n0 in range(0, CHUNK, width):
-                places = slice(n0, n0 + width)
-                values = slice(PACK * n0, PACK * (n0 + width))
-                h_copy(
-                    h_bf[:, values].rearrange("p (n t) -> p n t", t=PACK),
-                    h_banks[c][:, :, places].rearrange("p t n -> p n t"),
-                )
-                nc.vector.quantize_mx(
-                    out=h_codes[:, places].bitcast(FP8X4), scales=h_plane[:, places], in_=h_bf[:, values]
-                )
             nc.tensor.matmul_mx(
                 out=accs[c][:],
                 lhsT=w13_codes[:, N : 2 * N].bitcast(FP8X4),
                 lhsT_scale=planes[:, w3_plane_cols],
-                rhs=h_codes[:].bitcast(FP8X4),
-                rhs_scale=h_plane[:],
+                rhs=h_codes[c][:].bitcast(FP8X4),
+                rhs_scale=h_planes[c][:],
                 start=False,
                 stop=True,
             )

@@ -21,8 +21,8 @@ LIST_ROWS = 16
 CHUNK = 128
 GATHER = 256
 PAIR = 2
-HALF_H = H // 2
-WARM_PASSES = 2
+FIRST_PIECE = H
+WARM_PASSES = 3
 WARM_COLUMNS = 64
 WARM_WIDTH = 512
 
@@ -36,16 +36,12 @@ def tile_picked_phlora_none_p_kernel(
         keep = ctx.enter_context(tc.tile_pool(name="keep", bufs=1))
         psum = ctx.enter_context(tc.psum_pool(name="psum", bufs=1))
 
-        w2_rows = w2.rearrange("(p j) col -> p j col", j=PACK)
-        early_raw = keep.tile([P, PACK, HALF_H], F32, name="early_raw", align_bytes=64)
-        nc.sync.dma_start(early_raw[:], w2_rows[:, :, 0:HALF_H])
+        w2_rows = w2.rearrange("(p j) col -> p (j col)", j=PACK)
+        w2_raw = keep.tile([P, PACK * H], F32, name="w2_raw", tag="w2_raw_then_x_picked", align_bytes=64)
+        nc.sync.dma_start(w2_raw[:, 0:FIRST_PIECE], w2_rows[:, 0:FIRST_PIECE])
 
         offsets = keep.tile([P, S // LIST_ROWS], U16, name="offsets")
         nc.sync.dma_start(offsets[:], offs)
-
-        scale_table = keep.tile([P, T], U8, name="scale_table", align_bytes=64)
-        nc.vector.memset(scale_table[:].bitcast(I32), 0)
-        nc.sync.dma_start(scale_table[0:P:BLOCK_ROWS, :].bitcast(I32), x_scales[0].bitcast(I32))
 
         planes = keep.tile([P, S + 2 * N], U8, name="planes", align_bytes=64)
         w1_plane_cols = slice(S, S + N)
@@ -54,8 +50,11 @@ def tile_picked_phlora_none_p_kernel(
         nc.scalar.dma_start(planes[0:P:BLOCK_ROWS, w1_plane_cols].bitcast(I32), w1_scales[0].bitcast(I32))
         nc.scalar.dma_start(planes[0:P:BLOCK_ROWS, w3_plane_cols].bitcast(I32), w3_scales[0].bitcast(I32))
 
-        late_raw = keep.tile([P, PACK, HALF_H], F32, name="late_raw", tag="late_raw_then_x_picked", align_bytes=64)
-        nc.sync.dma_start(late_raw[:], w2_rows[:, :, HALF_H:H])
+        scale_table = keep.tile([P, T], U8, name="scale_table", align_bytes=64)
+        nc.vector.memset(scale_table[:].bitcast(I32), 0)
+        nc.sync.dma_start(scale_table[0:P:BLOCK_ROWS, :].bitcast(I32), x_scales[0].bitcast(I32))
+
+        nc.sync.dma_start(w2_raw[:, FIRST_PIECE : PACK * H], w2_rows[:, FIRST_PIECE : PACK * H])
         word_table = keep.tile([P, T], I32, name="word_table", align_bytes=64)
         nc.sync.dma_start(word_table[:], x_words[0].rearrange("p col byte -> p (col byte)").bitcast(I32))
 
@@ -73,32 +72,29 @@ def tile_picked_phlora_none_p_kernel(
 
         w2_codes_tile = keep.tile([P, H], U32, name="w2_codes", align_bytes=64)
         w2_plane_tile = keep.tile([P, H], U8, name="w2_plane", align_bytes=64)
-        half_m = P // 2
+        w2_src = w2_raw[:].rearrange("p (j m t) -> p m j t", j=PACK, t=PACK)
 
         def w2_operand(first, count):
             cols = slice(first, first + count)
             return w2_codes_tile[:, cols].bitcast(FP8X4), w2_plane_tile[:, cols]
 
-        def round_half(copy, raw, rounded, slots):
-            copy(
-                rounded[:].rearrange("p (t m j) -> p m j t", t=PACK, j=PACK)[:, :, :, slots],
-                raw[:].rearrange("p j (m t) -> p m j t", t=PACK)[:, :, :, slots],
-            )
+        def quantise_w2(rounded, first, count):
+            codes, plane = w2_operand(first, count)
+            start = PACK * (first % (PAIR * P))
+            nc.vector.quantize_mx(out=codes, scales=plane, in_=rounded[:, start : start + PACK * count])
 
-        def quantise_half(rounded, first_m):
-            for t in range(PACK):
-                codes, plane = w2_operand(P * t + first_m, half_m)
-                values = slice(t * half_m * PACK, (t + 1) * half_m * PACK)
-                nc.vector.quantize_mx(out=codes, scales=plane, in_=rounded[:, values])
-
-        early_bf = keep.tile([P, PACK * HALF_H], BF16, name="early_bf", align_bytes=64)
-        round_half(nc.scalar.copy, early_raw, early_bf, slice(0, PACK))
+        first_pair = keep.tile([P, PAIR * P * PACK], BF16, name="first_pair", align_bytes=64)
+        row_0 = w2_raw[:, 0:H].rearrange("p (m t) -> p t m", t=PACK)[:, 0:PAIR, :]
+        nc.scalar.copy(
+            first_pair[:].rearrange("p (t m j) -> p t m j", t=PAIR, j=PACK),
+            row_0.unsqueeze(3).to_broadcast([P, PAIR, P, PACK]),
+        )
 
         warm_codes = keep.tile([P, WARM_WIDTH], U32, name="warm_codes", align_bytes=64)
         warm_plane = keep.tile([P, WARM_WIDTH], U8, name="warm_plane", align_bytes=64)
-        for first in range(0, WARM_WIDTH, HALF_H):
-            cols = slice(first, first + HALF_H)
-            nc.vector.quantize_mx(out=warm_codes[:, cols].bitcast(FP8X4), scales=warm_plane[:, cols], in_=early_bf[:])
+        for first in range(0, WARM_WIDTH, PAIR * P):
+            cols = slice(first, first + PAIR * P)
+            nc.vector.quantize_mx(out=warm_codes[:, cols].bitcast(FP8X4), scales=warm_plane[:, cols], in_=first_pair[:])
         warm_bank = psum.tile([WARM_COLUMNS, WARM_WIDTH], F32, name="warm_bank", tag=f"acc{chunks - 2}")
         for warm_pass in range(WARM_PASSES):
             nc.tensor.matmul_mx(
@@ -110,14 +106,16 @@ def tile_picked_phlora_none_p_kernel(
                 start=True,
                 stop=True,
             )
-        quantise_half(early_bf, 0)
 
-        late_bf = keep.tile([P, PACK * HALF_H], BF16, name="late_bf", align_bytes=64)
-        round_half(nc.scalar.copy, late_raw, late_bf, slice(0, PAIR))
-        round_half(nc.scalar.copy, late_raw, late_bf, slice(PAIR, PACK))
-        quantise_half(late_bf, half_m)
+        second_pair = keep.tile([P, PAIR * P * PACK], BF16, name="second_pair", align_bytes=64)
+        first_dst = first_pair[:].rearrange("p (t m j) -> p m j t", t=PAIR, j=PACK)
+        second_dst = second_pair[:].rearrange("p (t m j) -> p m j t", t=PAIR, j=PACK)
+        nc.scalar.copy(second_dst, w2_src[:, :, :, PAIR:PACK])
+        nc.vector.tensor_copy(first_dst[:, :, 1:PACK, :], w2_src[:, :, 1:PACK, 0:PAIR])
+        quantise_w2(second_pair, PAIR * P, PAIR * P)
+        quantise_w2(first_pair, 0, PAIR * P)
 
-        x_picked = keep.tile([P, S], U32, name="x_picked", tag="late_raw_then_x_picked", align_bytes=64)
+        x_picked = keep.tile([P, S], U32, name="x_picked", tag="w2_raw_then_x_picked", align_bytes=64)
         for a in range(S // GATHER):
             nc.vector.tensor_copy(
                 x_picked[:, a * GATHER : (a + 1) * GATHER],
@@ -163,36 +161,39 @@ def tile_picked_phlora_none_p_kernel(
                 in_=h_bfs[index][:],
             )
 
-        accs = []
-        for c in range(chunks):
-            x_codes, x_plane = x_operand(c * CHUNK, CHUNK)
-            acc = psum.tile([P, CHUNK], F32, name=f"acc{c}", tag="h_bank0" if c == chunks - 1 else f"acc{c}")
+        def product(bank, weight_cols, plane_cols, codes, plane, start, stop):
             nc.tensor.matmul_mx(
-                out=acc[:],
-                lhsT=w13_codes[:, 0:N].bitcast(FP8X4),
-                lhsT_scale=planes[:, w1_plane_cols],
-                rhs=x_codes,
-                rhs_scale=x_plane,
-                start=True,
-                stop=False,
-            )
-            accs.append(acc)
-        for c in range(chunks):
-            nc.tensor.matmul_mx(
-                out=accs[c][:],
-                lhsT=w13_codes[:, N : 2 * N].bitcast(FP8X4),
-                lhsT_scale=planes[:, w3_plane_cols],
-                rhs=h_codes[c][:].bitcast(FP8X4),
-                rhs_scale=h_planes[c][:],
-                start=False,
-                stop=True,
+                out=bank,
+                lhsT=w13_codes[:, weight_cols].bitcast(FP8X4),
+                lhsT_scale=planes[:, plane_cols],
+                rhs=codes,
+                rhs_scale=plane,
+                start=start,
+                stop=stop,
             )
 
+        w1_cols, w3_cols = slice(0, N), slice(N, 2 * N)
+        whole = chunks - 1
+        accs = [psum.tile([P, CHUNK], F32, name=f"acc{c}", tag=f"acc{c}") for c in range(whole)]
+        for c in range(whole):
+            product(accs[c][:], w1_cols, w1_plane_cols, *x_operand(c * CHUNK, CHUNK), True, False)
+        w1_bank = psum.tile([P, CHUNK], F32, name="w1_bank", tag="h_bank0")
+        for first, count in pieces[whole:]:
+            places = slice(first % CHUNK, first % CHUNK + count)
+            product(w1_bank[:, places], w1_cols, w1_plane_cols, *x_operand(first, count), True, True)
+        w1_term = keep.tile([P, CHUNK], F32, name="w1_term")
+        nc.scalar.copy(w1_term[:], w1_bank[:])
+
         result = keep.tile([P, S], F32, name="result")
-        store_from = {1: 0, 2: 2 * CHUNK, 3: 3 * CHUNK}
-        for c in range(chunks):
-            out_copy = nc.vector.tensor_copy if c == chunks - 1 else nc.scalar.copy
-            out_copy(result[:, c * CHUNK : (c + 1) * CHUNK], accs[c][:])
-            if c in store_from:
-                stored = slice(store_from[c], (c + 1) * CHUNK)
-                nc.sync.dma_start(out[:, stored], result[:, stored])
+        for c in range(whole):
+            product(accs[c][:], w3_cols, w3_plane_cols, h_codes[c][:].bitcast(FP8X4), h_planes[c][:], False, True)
+            nc.scalar.copy(result[:, c * CHUNK : (c + 1) * CHUNK], accs[c][:])
+        for index, (first, count) in enumerate(pieces[whole:]):
+            places = slice(first % CHUNK, first % CHUNK + count)
+            w3_bank = psum.tile([P, count], F32, name=f"w3_bank{index}", tag=f"h_bank{index + 1}")
+            codes, plane = h_codes[whole][:, places].bitcast(FP8X4), h_planes[whole][:, places]
+            product(w3_bank[:], w3_cols, w3_plane_cols, codes, plane, True, True)
+            nc.vector.tensor_add(result[:, first : first + count], w3_bank[:], w1_term[:, places])
+
+        for stored in (slice(0, 2 * CHUNK), slice(2 * CHUNK, 3 * CHUNK), slice(3 * CHUNK, S)):
+            nc.sync.dma_start(out[:, stored], result[:, stored])

@@ -21,7 +21,7 @@ LIST_ROWS = 16
 CHUNK = 128
 GATHER = 256
 PAIR = 2
-FIRST_PIECE = H
+FIRST_PIECE = 768
 WARM_PASSES = 3
 WARM_COLUMNS = 64
 WARM_WIDTH = 512
@@ -43,16 +43,17 @@ def tile_picked_phlora_none_p_kernel(
         offsets = keep.tile([P, S // LIST_ROWS], U16, name="offsets")
         nc.sync.dma_start(offsets[:], offs)
 
-        planes = keep.tile([P, S + 2 * N], U8, name="planes", align_bytes=64)
-        w1_plane_cols = slice(S, S + N)
-        w3_plane_cols = slice(S + N, S + 2 * N)
-        nc.vector.memset(planes[:, S : S + 2 * N].bitcast(I32), 0)
-        nc.scalar.dma_start(planes[0:P:BLOCK_ROWS, w1_plane_cols].bitcast(I32), w1_scales[0].bitcast(I32))
-        nc.scalar.dma_start(planes[0:P:BLOCK_ROWS, w3_plane_cols].bitcast(I32), w3_scales[0].bitcast(I32))
-
         scale_table = keep.tile([P, T], U8, name="scale_table", align_bytes=64)
         nc.vector.memset(scale_table[:].bitcast(I32), 0)
         nc.sync.dma_start(scale_table[0:P:BLOCK_ROWS, :].bitcast(I32), x_scales[0].bitcast(I32))
+
+        staged = keep.tile([P, S + 2 * N], U8, name="staged", align_bytes=64)
+        planes = keep.tile([P, S + 2 * N], U8, name="planes", align_bytes=64)
+        w1_plane_cols = slice(S, S + N)
+        w3_plane_cols = slice(S + N, S + 2 * N)
+        nc.scalar.dma_start(staged[0:P:BLOCK_ROWS, w1_plane_cols].bitcast(I32), w1_scales[0].bitcast(I32))
+        nc.scalar.dma_start(staged[0:P:BLOCK_ROWS, w3_plane_cols].bitcast(I32), w3_scales[0].bitcast(I32))
+        nc.vector.memset(planes[:].bitcast(I32), 0)
 
         nc.sync.dma_start(w2_raw[:, FIRST_PIECE : PACK * H], w2_rows[:, FIRST_PIECE : PACK * H])
         word_table = keep.tile([P, T], I32, name="word_table", align_bytes=64)
@@ -60,10 +61,10 @@ def tile_picked_phlora_none_p_kernel(
 
         scales_picked = keep.tile([P, S], U8, name="scales_picked", tag="scales_then_w13", align_bytes=64)
         nc.vector.tensor_copy(scales_picked[:], scale_table[:].indirect(offsets[:]))
-        nc.vector.tensor_copy(planes[:, 0:S].bitcast(I32), scales_picked[:].bitcast(I32))
-        for e in range(1, QUADRANT // BLOCK_ROWS):
+        nc.vector.tensor_copy(staged[:, 0:S].bitcast(I32), scales_picked[:].bitcast(I32))
+        for e in range(QUADRANT // BLOCK_ROWS):
             nc.sync.dma_start(
-                planes[e:P:QUADRANT, :].bitcast(I32), planes[BLOCK_ROWS * e : P : QUADRANT, :].bitcast(I32)
+                planes[e:P:QUADRANT, :].bitcast(I32), staged[BLOCK_ROWS * e : P : QUADRANT, :].bitcast(I32)
             )
 
         w13_codes = keep.tile([P, 2 * N], I32, name="w13_codes", tag="scales_then_w13", align_bytes=64)
@@ -107,13 +108,18 @@ def tile_picked_phlora_none_p_kernel(
                 stop=True,
             )
 
-        second_pair = keep.tile([P, PAIR * P * PACK], BF16, name="second_pair", align_bytes=64)
         first_dst = first_pair[:].rearrange("p (t m j) -> p m j t", t=PAIR, j=PACK)
+        halves = (slice(0, P // 2), slice(P // 2, P))
+        for m_half in halves:
+            nc.vector.tensor_copy(first_dst[:, m_half, 1:PACK, :], w2_src[:, m_half, 1:PACK, 0:PAIR])
+        for m_half in halves:
+            for t in range(PAIR):
+                quantise_w2(first_pair, P * t + m_half.start, P // 2)
+
+        second_pair = keep.tile([P, PAIR * P * PACK], BF16, name="second_pair", align_bytes=64)
         second_dst = second_pair[:].rearrange("p (t m j) -> p m j t", t=PAIR, j=PACK)
         nc.scalar.copy(second_dst, w2_src[:, :, :, PAIR:PACK])
-        nc.vector.tensor_copy(first_dst[:, :, 1:PACK, :], w2_src[:, :, 1:PACK, 0:PAIR])
         quantise_w2(second_pair, PAIR * P, PAIR * P)
-        quantise_w2(first_pair, 0, PAIR * P)
 
         x_picked = keep.tile([P, S], U32, name="x_picked", tag="w2_raw_then_x_picked", align_bytes=64)
         for a in range(S // GATHER):

@@ -21,7 +21,7 @@ LIST_ROWS = 16
 CHUNK = 128
 GATHER = 256
 PAIR = 2
-FIRST_PIECE = 768
+FIRST_PIECE = 640
 WARM_PASSES = 3
 WARM_COLUMNS = 64
 WARM_WIDTH = 512

@@ -21,10 +21,10 @@ LIST_ROWS = 16
 CHUNK = 128
 GATHER = 256
 PAIR = 2
-FIRST_PIECE = 640
-WARM_PASSES = 3
-WARM_COLUMNS = 64
-WARM_WIDTH = 512
+FIRST_PIECE = 896
+WARM_WIDTHS = (512, 512, 128)
+WARM_COLUMNS = 32
+WARM_WIDTH = max(WARM_WIDTHS)
 
 
 def tile_picked_phlora_none_p_kernel(
@@ -97,13 +97,13 @@ def tile_picked_phlora_none_p_kernel(
             cols = slice(first, first + PAIR * P)
             nc.vector.quantize_mx(out=warm_codes[:, cols].bitcast(FP8X4), scales=warm_plane[:, cols], in_=first_pair[:])
         warm_bank = psum.tile([WARM_COLUMNS, WARM_WIDTH], F32, name="warm_bank", tag=f"acc{chunks - 2}")
-        for warm_pass in range(WARM_PASSES):
+        for width in WARM_WIDTHS:
             nc.tensor.matmul_mx(
-                out=warm_bank[:],
+                out=warm_bank[:, 0:width],
                 lhsT=warm_codes[:, 0:WARM_COLUMNS].bitcast(FP8X4),
                 lhsT_scale=warm_plane[:, 0:WARM_COLUMNS],
-                rhs=warm_codes[:].bitcast(FP8X4),
-                rhs_scale=warm_plane[:],
+                rhs=warm_codes[:, 0:width].bitcast(FP8X4),
+                rhs_scale=warm_plane[:, 0:width],
                 start=True,
                 stop=True,
             )

@@ -37,18 +37,18 @@ def tile_picked_phlora_none_p_kernel(
         psum = ctx.enter_context(tc.psum_pool(name="psum", bufs=1))
 
         w2_rows = w2.rearrange("(p j) col -> p (j col)", j=PACK)
-        w2_raw = keep.tile([P, PACK * H], F32, name="w2_raw", tag="w2_raw_then_x_picked", align_bytes=64)
+        w2_raw = keep.tile([P, PACK * H], F32, name="w2_raw", tag="w2_raw_then_x_picked", align_bytes=256)
         nc.sync.dma_start(w2_raw[:, 0:FIRST_PIECE], w2_rows[:, 0:FIRST_PIECE])
 
         offsets = keep.tile([P, S // LIST_ROWS], U16, name="offsets")
         nc.sync.dma_start(offsets[:], offs)
 
-        scale_table = keep.tile([P, T], U8, name="scale_table", align_bytes=64)
+        scale_table = keep.tile([P, T], U8, name="scale_table", align_bytes=256)
         nc.vector.memset(scale_table[:].bitcast(I32), 0)
         nc.sync.dma_start(scale_table[0:P:BLOCK_ROWS, :].bitcast(I32), x_scales[0].bitcast(I32))
 
-        staged = keep.tile([P, S + 2 * N], U8, name="staged", align_bytes=64)
-        planes = keep.tile([P, S + 2 * N], U8, name="planes", align_bytes=64)
+        staged = keep.tile([P, S + 2 * N], U8, name="staged", align_bytes=256)
+        planes = keep.tile([P, S + 2 * N], U8, name="planes", align_bytes=256)
         w1_plane_cols = slice(S, S + N)
         w3_plane_cols = slice(S + N, S + 2 * N)
         nc.scalar.dma_start(staged[0:P:BLOCK_ROWS, w1_plane_cols].bitcast(I32), w1_scales[0].bitcast(I32))
@@ -56,10 +56,10 @@ def tile_picked_phlora_none_p_kernel(
         nc.vector.memset(planes[:].bitcast(I32), 0)
 
         nc.sync.dma_start(w2_raw[:, FIRST_PIECE : PACK * H], w2_rows[:, FIRST_PIECE : PACK * H])
-        word_table = keep.tile([P, T], I32, name="word_table", align_bytes=64)
+        word_table = keep.tile([P, T], I32, name="word_table", align_bytes=256)
         nc.sync.dma_start(word_table[:], x_words[0].rearrange("p col byte -> p (col byte)").bitcast(I32))
 
-        scales_picked = keep.tile([P, S], U8, name="scales_picked", tag="scales_then_w13", align_bytes=64)
+        scales_picked = keep.tile([P, S], U8, name="scales_picked", tag="scales_then_w13", align_bytes=256)
         nc.vector.tensor_copy(scales_picked[:], scale_table[:].indirect(offsets[:]))
         nc.vector.tensor_copy(staged[:, 0:S].bitcast(I32), scales_picked[:].bitcast(I32))
         for e in range(QUADRANT // BLOCK_ROWS):
@@ -67,12 +67,12 @@ def tile_picked_phlora_none_p_kernel(
                 planes[e:P:QUADRANT, :].bitcast(I32), staged[BLOCK_ROWS * e : P : QUADRANT, :].bitcast(I32)
             )
 
-        w13_codes = keep.tile([P, 2 * N], I32, name="w13_codes", tag="scales_then_w13", align_bytes=64)
+        w13_codes = keep.tile([P, 2 * N], I32, name="w13_codes", tag="scales_then_w13", align_bytes=256)
         nc.sync.dma_start(w13_codes[:, 0:N], w1_words[0].rearrange("p col byte -> p (col byte)").bitcast(I32))
         nc.sync.dma_start(w13_codes[:, N : 2 * N], w3_words[0].rearrange("p col byte -> p (col byte)").bitcast(I32))
 
-        w2_codes_tile = keep.tile([P, H], U32, name="w2_codes", align_bytes=64)
-        w2_plane_tile = keep.tile([P, H], U8, name="w2_plane", align_bytes=64)
+        w2_codes_tile = keep.tile([P, H], U32, name="w2_codes", align_bytes=256)
+        w2_plane_tile = keep.tile([P, H], U8, name="w2_plane", align_bytes=256)
         w2_src = w2_raw[:].rearrange("p (j m t) -> p m j t", j=PACK, t=PACK)
 
         def w2_operand(first, count):
@@ -84,15 +84,15 @@ def tile_picked_phlora_none_p_kernel(
             start = PACK * (first % (PAIR * P))
             nc.vector.quantize_mx(out=codes, scales=plane, in_=rounded[:, start : start + PACK * count])
 
-        first_pair = keep.tile([P, PAIR * P * PACK], BF16, name="first_pair", align_bytes=64)
+        first_pair = keep.tile([P, PAIR * P * PACK], BF16, name="first_pair", align_bytes=256)
         row_0 = w2_raw[:, 0:H].rearrange("p (m t) -> p t m", t=PACK)[:, 0:PAIR, :]
         nc.scalar.copy(
             first_pair[:].rearrange("p (t m j) -> p t m j", t=PAIR, j=PACK),
             row_0.unsqueeze(3).to_broadcast([P, PAIR, P, PACK]),
         )
 
-        warm_codes = keep.tile([P, WARM_WIDTH], U32, name="warm_codes", align_bytes=64)
-        warm_plane = keep.tile([P, WARM_WIDTH], U8, name="warm_plane", align_bytes=64)
+        warm_codes = keep.tile([P, WARM_WIDTH], U32, name="warm_codes", align_bytes=256)
+        warm_plane = keep.tile([P, WARM_WIDTH], U8, name="warm_plane", align_bytes=256)
         for first in range(0, WARM_WIDTH, PAIR * P):
             cols = slice(first, first + PAIR * P)
             nc.vector.quantize_mx(out=warm_codes[:, cols].bitcast(FP8X4), scales=warm_plane[:, cols], in_=first_pair[:])
@@ -116,12 +116,12 @@ def tile_picked_phlora_none_p_kernel(
             for t in range(PAIR):
                 quantise_w2(first_pair, P * t + m_half.start, P // 2)
 
-        second_pair = keep.tile([P, PAIR * P * PACK], BF16, name="second_pair", align_bytes=64)
+        second_pair = keep.tile([P, PAIR * P * PACK], BF16, name="second_pair", align_bytes=256)
         second_dst = second_pair[:].rearrange("p (t m j) -> p m j t", t=PAIR, j=PACK)
         nc.scalar.copy(second_dst, w2_src[:, :, :, PAIR:PACK])
         quantise_w2(second_pair, PAIR * P, PAIR * P)
 
-        x_picked = keep.tile([P, S], U32, name="x_picked", tag="w2_raw_then_x_picked", align_bytes=64)
+        x_picked = keep.tile([P, S], U32, name="x_picked", tag="w2_raw_then_x_picked", align_bytes=256)
         for a in range(S // GATHER):
             nc.vector.tensor_copy(
                 x_picked[:, a * GATHER : (a + 1) * GATHER],
@@ -151,11 +151,11 @@ def tile_picked_phlora_none_p_kernel(
                 )
             h_banks.append(h_bank)
 
-        h_codes = [keep.tile([P, CHUNK], U32, name=f"h_codes{c}", align_bytes=64) for c in range(chunks)]
-        h_planes = [keep.tile([P, CHUNK], U8, name=f"h_plane{c}", align_bytes=64) for c in range(chunks)]
+        h_codes = [keep.tile([P, CHUNK], U32, name=f"h_codes{c}", align_bytes=256) for c in range(chunks)]
+        h_planes = [keep.tile([P, CHUNK], U8, name=f"h_plane{c}", align_bytes=256) for c in range(chunks)]
         h_bfs = []
         for index, (first, count) in enumerate(pieces):
-            h_bf = keep.tile([P, count * PACK], BF16, name=f"h_bf{index}", align_bytes=64)
+            h_bf = keep.tile([P, count * PACK], BF16, name=f"h_bf{index}", align_bytes=256)
             h_copy = nc.vector.tensor_copy if index % 2 else nc.scalar.copy
             h_copy(h_bf[:].rearrange("p (n t) -> p n t", t=PACK), h_banks[index][:].rearrange("p t n -> p n t"))
             h_bfs.append(h_bf)
@@ -179,27 +179,15 @@ def tile_picked_phlora_none_p_kernel(
             )
 
         w1_cols, w3_cols = slice(0, N), slice(N, 2 * N)
-        whole = chunks - 1
-        accs = [psum.tile([P, CHUNK], F32, name=f"acc{c}", tag=f"acc{c}") for c in range(whole)]
-        for c in range(whole):
+        tags = [f"acc{c}" for c in range(chunks - 1)] + ["h_bank0"]
+        accs = [psum.tile([P, CHUNK], F32, name=f"acc{c}", tag=tags[c]) for c in range(chunks)]
+        for c in range(chunks):
             product(accs[c][:], w1_cols, w1_plane_cols, *x_operand(c * CHUNK, CHUNK), True, False)
-        w1_bank = psum.tile([P, CHUNK], F32, name="w1_bank", tag="h_bank0")
-        for first, count in pieces[whole:]:
-            places = slice(first % CHUNK, first % CHUNK + count)
-            product(w1_bank[:, places], w1_cols, w1_plane_cols, *x_operand(first, count), True, True)
-        w1_term = keep.tile([P, CHUNK], F32, name="w1_term")
-        nc.scalar.copy(w1_term[:], w1_bank[:])
-
         result = keep.tile([P, S], F32, name="result")
-        for c in range(whole):
+        for c in range(chunks):
             product(accs[c][:], w3_cols, w3_plane_cols, h_codes[c][:].bitcast(FP8X4), h_planes[c][:], False, True)
-            nc.scalar.copy(result[:, c * CHUNK : (c + 1) * CHUNK], accs[c][:])
-        for index, (first, count) in enumerate(pieces[whole:]):
-            places = slice(first % CHUNK, first % CHUNK + count)
-            w3_bank = psum.tile([P, count], F32, name=f"w3_bank{index}", tag=f"h_bank{index + 1}")
-            codes, plane = h_codes[whole][:, places].bitcast(FP8X4), h_planes[whole][:, places]
-            product(w3_bank[:], w3_cols, w3_plane_cols, codes, plane, True, True)
-            nc.vector.tensor_add(result[:, first : first + count], w3_bank[:], w1_term[:, places])
+            out_copy = nc.vector.tensor_copy if c == chunks - 1 else nc.scalar.copy
+            out_copy(result[:, c * CHUNK : (c + 1) * CHUNK], accs[c][:])
 
         for stored in (slice(0, 2 * CHUNK), slice(2 * CHUNK, 3 * CHUNK), slice(3 * CHUNK, S)):
             nc.sync.dma_start(out[:, stored], result[:, stored])

@@ -109,10 +109,14 @@ def tile_picked_phlora_none_p_kernel(
             )
 
         first_dst = first_pair[:].rearrange("p (t m j) -> p m j t", t=PAIR, j=PACK)
-        halves = (slice(0, P // 2), slice(P // 2, P))
-        for m_half in halves:
-            nc.vector.tensor_copy(first_dst[:, m_half, 1:PACK, :], w2_src[:, m_half, 1:PACK, 0:PAIR])
-        for m_half in halves:
+        quarter = P // 4
+        for round_rows, m_part in (
+            (nc.scalar.copy, slice(3 * quarter, P)),
+            (nc.vector.tensor_copy, slice(2 * quarter, 3 * quarter)),
+            (nc.vector.tensor_copy, slice(0, 2 * quarter)),
+        ):
+            round_rows(first_dst[:, m_part, 1:PACK, :], w2_src[:, m_part, 1:PACK, 0:PAIR])
+        for m_half in (slice(P // 2, P), slice(0, P // 2)):
             for t in range(PAIR):
                 quantise_w2(first_pair, P * t + m_half.start, P // 2)
 
@@ -189,5 +193,5 @@ def tile_picked_phlora_none_p_kernel(
             out_copy = nc.vector.tensor_copy if c == chunks - 1 else nc.scalar.copy
             out_copy(result[:, c * CHUNK : (c + 1) * CHUNK], accs[c][:])
 
-        for stored in (slice(0, 2 * CHUNK), slice(2 * CHUNK, 3 * CHUNK), slice(3 * CHUNK, S)):
+        for stored in (slice(0, 2 * CHUNK), slice(2 * CHUNK, S)):
             nc.sync.dma_start(out[:, stored], result[:, stored])

@@ -79,23 +79,27 @@ def tile_picked_phlora_none_p_kernel(
             cols = slice(first, first + count)
             return w2_codes_tile[:, cols].bitcast(FP8X4), w2_plane_tile[:, cols]
 
-        def quantise_w2(rounded, first, count):
-            codes, plane = w2_operand(first, count)
-            start = PACK * (first % (PAIR * P))
-            nc.vector.quantize_mx(out=codes, scales=plane, in_=rounded[:, start : start + PACK * count])
+        def quantise_w2(rounded, first):
+            codes, plane = w2_operand(first, rounded.shape[1] // PACK)
+            nc.vector.quantize_mx(out=codes, scales=plane, in_=rounded)
 
-        first_pair = keep.tile([P, PAIR * P * PACK], BF16, name="first_pair", align_bytes=256)
-        row_0 = w2_raw[:, 0:H].rearrange("p (m t) -> p t m", t=PACK)[:, 0:PAIR, :]
+        half_m = P // 2
+        half_run = PAIR * half_m * PACK
+        first_pair = keep.tile([P, 2 * half_run], BF16, name="first_pair", align_bytes=256)
+        row_0 = w2_raw[:, 0:H].rearrange("p (h m t) -> p h t m", h=2, t=PACK)[:, :, 0:PAIR, :]
         nc.scalar.copy(
-            first_pair[:].rearrange("p (t m j) -> p t m j", t=PAIR, j=PACK),
-            row_0.unsqueeze(3).to_broadcast([P, PAIR, P, PACK]),
+            first_pair[:].rearrange("p (h t m j) -> p h t m j", h=2, t=PAIR, j=PACK),
+            row_0.unsqueeze(4).to_broadcast([P, 2, PAIR, half_m, PACK]),
         )
 
         warm_codes = keep.tile([P, WARM_WIDTH], U32, name="warm_codes", align_bytes=256)
         warm_plane = keep.tile([P, WARM_WIDTH], U8, name="warm_plane", align_bytes=256)
-        for first in range(0, WARM_WIDTH, PAIR * P):
-            cols = slice(first, first + PAIR * P)
-            nc.vector.quantize_mx(out=warm_codes[:, cols].bitcast(FP8X4), scales=warm_plane[:, cols], in_=first_pair[:])
+        for first, last, source in ((0, 2 * P, 0), (2 * P, 3 * P, half_run), (3 * P, 4 * P, half_run)):
+            nc.vector.quantize_mx(
+                out=warm_codes[:, first:last].bitcast(FP8X4),
+                scales=warm_plane[:, first:last],
+                in_=first_pair[:, source : 2 * half_run],
+            )
         warm_bank = psum.tile([WARM_COLUMNS, WARM_WIDTH], F32, name="warm_bank", tag=f"acc{chunks - 2}")
         for width in WARM_WIDTHS:
             nc.tensor.matmul_mx(
@@ -108,22 +112,29 @@ def tile_picked_phlora_none_p_kernel(
                 stop=True,
             )
 
-        first_dst = first_pair[:].rearrange("p (t m j) -> p m j t", t=PAIR, j=PACK)
-        quarter = P // 4
-        for round_rows, m_part in (
-            (nc.scalar.copy, slice(3 * quarter, P)),
-            (nc.vector.tensor_copy, slice(2 * quarter, 3 * quarter)),
-            (nc.vector.tensor_copy, slice(0, 2 * quarter)),
-        ):
-            round_rows(first_dst[:, m_part, 1:PACK, :], w2_src[:, m_part, 1:PACK, 0:PAIR])
-        for m_half in (slice(P // 2, P), slice(0, P // 2)):
-            for t in range(PAIR):
-                quantise_w2(first_pair, P * t + m_half.start, P // 2)
-
         second_pair = keep.tile([P, PAIR * P * PACK], BF16, name="second_pair", align_bytes=256)
         second_dst = second_pair[:].rearrange("p (t m j) -> p m j t", t=PAIR, j=PACK)
         nc.scalar.copy(second_dst, w2_src[:, :, :, PAIR:PACK])
-        quantise_w2(second_pair, PAIR * P, PAIR * P)
+        first_dst = first_pair[:].rearrange("p (h t m j) -> p h m j t", h=2, t=PAIR, j=PACK)
+        quarter_m = P // 4
+        for round_rows, first, count in (
+            (nc.vector.tensor_copy, 0, half_m),
+            (nc.vector.tensor_copy, half_m, quarter_m),
+            (nc.scalar.copy, half_m + quarter_m, quarter_m),
+        ):
+            within = slice(first % half_m, first % half_m + count)
+            round_rows(
+                first_dst[:, first // half_m, within, 1:PACK, :], w2_src[:, first : first + count, 1:PACK, 0:PAIR]
+            )
+
+        def quantise_half(h):
+            for t in range(PAIR):
+                start = h * half_run + t * half_m * PACK
+                quantise_w2(first_pair[:, start : start + half_m * PACK], t * P + h * half_m)
+
+        quantise_half(0)
+        quantise_w2(second_pair[:], PAIR * P)
+        quantise_half(1)
 
         x_picked = keep.tile([P, S], U32, name="x_picked", tag="w2_raw_then_x_picked", align_bytes=256)
         for a in range(S // GATHER):
@@ -190,7 +201,7 @@ def tile_picked_phlora_none_p_kernel(
         result = keep.tile([P, S], F32, name="result")
         for c in range(chunks):
             product(accs[c][:], w3_cols, w3_plane_cols, h_codes[c][:].bitcast(FP8X4), h_planes[c][:], False, True)
-            out_copy = nc.vector.tensor_copy if c == chunks - 1 else nc.scalar.copy
+            out_copy = nc.vector.tensor_copy if c >= chunks // 2 else nc.scalar.copy
             out_copy(result[:, c * CHUNK : (c + 1) * CHUNK], accs[c][:])
 
         for stored in (slice(0, 2 * CHUNK), slice(2 * CHUNK, S)):

from contextlib import ExitStack

import concourse.mybir as mybir

K, T, S, H, N = 512, 2048, 512, 512, 128
FLOPS = 2 * K * H * S + 2 * K * N * S + 2 * H * N * S

F32 = mybir.dt.float32
BF16 = mybir.dt.bfloat16
I32 = mybir.dt.int32
U32 = mybir.dt.uint32
U16 = mybir.dt.uint16
U8 = mybir.dt.uint8
FP8X4 = mybir.dt.float8_e4m3fn_x4

P = 128
PACK = 4
BLOCK_ROWS = 8
QUADRANT = 32
LIST_ROWS = 16
CHUNK = 128
GATHER = 256
PAIR = 2
FIRST_PIECE = 896
WARM_WIDTHS = (512, 512, 128)
WARM_COLUMNS = 32
WARM_WIDTH = max(WARM_WIDTHS)


def tile_picked_phlora_none_p_kernel(
    tc, x_words, x_scales, w1_words, w1_scales, w2, w3_words, w3_scales, offs, out
):
    nc = tc.nc
    chunks = S // CHUNK
    with ExitStack() as ctx:
        keep = ctx.enter_context(tc.tile_pool(name="keep", bufs=1))
        psum = ctx.enter_context(tc.psum_pool(name="psum", bufs=1))

        w2_rows = w2.rearrange("(p j) col -> p (j col)", j=PACK)
        w2_raw = keep.tile([P, PACK * H], F32, name="w2_raw", tag="w2_raw_then_x_picked", align_bytes=256)
        nc.sync.dma_start(w2_raw[:, 0:FIRST_PIECE], w2_rows[:, 0:FIRST_PIECE])

        offsets = keep.tile([P, S // LIST_ROWS], U16, name="offsets")
        nc.sync.dma_start(offsets[:], offs)

        scale_table = keep.tile([P, T], U8, name="scale_table", align_bytes=256)
        nc.vector.memset(scale_table[:].bitcast(I32), 0)
        nc.sync.dma_start(scale_table[0:P:BLOCK_ROWS, :].bitcast(I32), x_scales[0].bitcast(I32))

        staged = keep.tile([P, S + 2 * N], U8, name="staged", align_bytes=256)
        planes = keep.tile([P, S + 2 * N], U8, name="planes", align_bytes=256)
        w1_plane_cols = slice(S, S + N)
        w3_plane_cols = slice(S + N, S + 2 * N)
        nc.scalar.dma_start(staged[0:P:BLOCK_ROWS, w1_plane_cols].bitcast(I32), w1_scales[0].bitcast(I32))
        nc.scalar.dma_start(staged[0:P:BLOCK_ROWS, w3_plane_cols].bitcast(I32), w3_scales[0].bitcast(I32))
        nc.vector.memset(planes[:].bitcast(I32), 0)

        nc.sync.dma_start(w2_raw[:, FIRST_PIECE : PACK * H], w2_rows[:, FIRST_PIECE : PACK * H])
        word_table = keep.tile([P, T], I32, name="word_table", align_bytes=256)
        nc.sync.dma_start(word_table[:], x_words[0].rearrange("p col byte -> p (col byte)").bitcast(I32))

        scales_picked = keep.tile([P, S], U8, name="scales_picked", tag="scales_then_w13", align_bytes=256)
        nc.vector.tensor_copy(scales_picked[:], scale_table[:].indirect(offsets[:]))
        nc.vector.tensor_copy(staged[:, 0:S].bitcast(I32), scales_picked[:].bitcast(I32))
        for e in range(QUADRANT // BLOCK_ROWS):
            nc.sync.dma_start(
                planes[e:P:QUADRANT, :].bitcast(I32), staged[BLOCK_ROWS * e : P : QUADRANT, :].bitcast(I32)
            )

        w13_codes = keep.tile([P, 2 * N], I32, name="w13_codes", tag="scales_then_w13", align_bytes=256)
        nc.sync.dma_start(w13_codes[:, 0:N], w1_words[0].rearrange("p col byte -> p (col byte)").bitcast(I32))
        nc.sync.dma_start(w13_codes[:, N : 2 * N], w3_words[0].rearrange("p col byte -> p (col byte)").bitcast(I32))

        w2_codes_tile = keep.tile([P, H], U32, name="w2_codes", align_bytes=256)
        w2_plane_tile = keep.tile([P, H], U8, name="w2_plane", align_bytes=256)
        w2_src = w2_raw[:].rearrange("p (j m t) -> p m j t", j=PACK, t=PACK)

        def w2_operand(first, count):
            cols = slice(first, first + count)
            return w2_codes_tile[:, cols].bitcast(FP8X4), w2_plane_tile[:, cols]

        def quantise_w2(rounded, first):
            codes, plane = w2_operand(first, rounded.shape[1] // PACK)
            nc.vector.quantize_mx(out=codes, scales=plane, in_=rounded)

        half_m = P // 2
        half_run = PAIR * half_m * PACK
        first_pair = keep.tile([P, 2 * half_run], BF16, name="first_pair", align_bytes=256)
        row_0 = w2_raw[:, 0:H].rearrange("p (h m t) -> p h t m", h=2, t=PACK)[:, :, 0:PAIR, :]
        nc.scalar.copy(
            first_pair[:].rearrange("p (h t m j) -> p h t m j", h=2, t=PAIR, j=PACK),
            row_0.unsqueeze(4).to_broadcast([P, 2, PAIR, half_m, PACK]),
        )

        warm_codes = keep.tile([P, WARM_WIDTH], U32, name="warm_codes", align_bytes=256)
        warm_plane = keep.tile([P, WARM_WIDTH], U8, name="warm_plane", align_bytes=256)
        for first, last, source in ((0, 2 * P, 0), (2 * P, 3 * P, half_run), (3 * P, 4 * P, half_run)):
            nc.vector.quantize_mx(
                out=warm_codes[:, first:last].bitcast(FP8X4),
                scales=warm_plane[:, first:last],
                in_=first_pair[:, source : 2 * half_run],
            )
        warm_bank = psum.tile([WARM_COLUMNS, WARM_WIDTH], F32, name="warm_bank", tag=f"acc{chunks - 2}")
        for width in WARM_WIDTHS:
            nc.tensor.matmul_mx(
                out=warm_bank[:, 0:width],
                lhsT=warm_codes[:, 0:WARM_COLUMNS].bitcast(FP8X4),
                lhsT_scale=warm_plane[:, 0:WARM_COLUMNS],
                rhs=warm_codes[:, 0:width].bitcast(FP8X4),
                rhs_scale=warm_plane[:, 0:width],
                start=True,
                stop=True,
            )

        second_pair = keep.tile([P, PAIR * P * PACK], BF16, name="second_pair", align_bytes=256)
        second_dst = second_pair[:].rearrange("p (t m j) -> p m j t", t=PAIR, j=PACK)
        nc.scalar.copy(second_dst, w2_src[:, :, :, PAIR:PACK])
        first_dst = first_pair[:].rearrange("p (h t m j) -> p h m j t", h=2, t=PAIR, j=PACK)
        quarter_m = P // 4
        for round_rows, first, count in (
            (nc.vector.tensor_copy, 0, half_m),
            (nc.vector.tensor_copy, half_m, quarter_m),
            (nc.scalar.copy, half_m + quarter_m, quarter_m),
        ):
            within = slice(first % half_m, first % half_m + count)
            round_rows(
                first_dst[:, first // half_m, within, 1:PACK, :], w2_src[:, first : first + count, 1:PACK, 0:PAIR]
            )

        def quantise_half(h):
            for t in range(PAIR):
                start = h * half_run + t * half_m * PACK
                quantise_w2(first_pair[:, start : start + half_m * PACK], t * P + h * half_m)

        quantise_half(0)
        quantise_w2(second_pair[:], PAIR * P)
        quantise_half(1)

        x_picked = keep.tile([P, S], U32, name="x_picked", tag="w2_raw_then_x_picked", align_bytes=256)
        for a in range(S // GATHER):
            nc.vector.tensor_copy(
                x_picked[:, a * GATHER : (a + 1) * GATHER],
                word_table[:].bitcast(U32).indirect(offsets[:, a * GATHER // LIST_ROWS : (a + 1) * GATHER // LIST_ROWS]),
            )

        def x_operand(first, count):
            cols = slice(first, first + count)
            return x_picked[:, cols].bitcast(FP8X4), planes[:, cols]

        half = CHUNK // 2
        pieces = [(c * CHUNK, CHUNK) for c in range(chunks - 1)] + [(S - CHUNK, half), (S - half, half)]
        h_banks = []
        for index, (first, count) in enumerate(pieces):
            x_codes, x_plane = x_operand(first, count)
            h_bank = psum.tile([P, PACK, count], F32, name=f"h_bank{index}", tag=f"h_bank{index}")
            for t in range(PACK):
                w2_codes, w2_plane = w2_operand(t * P, P)
                nc.tensor.matmul_mx(
                    out=h_bank[:, t, :],
                    lhsT=w2_codes,
                    lhsT_scale=w2_plane,
                    rhs=x_codes,
                    rhs_scale=x_plane,
                    start=True,
                    stop=True,
                )
            h_banks.append(h_bank)

        h_codes = [keep.tile([P, CHUNK], U32, name=f"h_codes{c}", align_bytes=256) for c in range(chunks)]
        h_planes = [keep.tile([P, CHUNK], U8, name=f"h_plane{c}", align_bytes=256) for c in range(chunks)]
        h_bfs = []
        for index, (first, count) in enumerate(pieces):
            h_bf = keep.tile([P, count * PACK], BF16, name=f"h_bf{index}", align_bytes=256)
            h_copy = nc.vector.tensor_copy if index % 2 else nc.scalar.copy
            h_copy(h_bf[:].rearrange("p (n t) -> p n t", t=PACK), h_banks[index][:].rearrange("p t n -> p n t"))
            h_bfs.append(h_bf)
        for index, (first, count) in enumerate(pieces):
            places = slice(first % CHUNK, first % CHUNK + count)
            nc.vector.quantize_mx(
                out=h_codes[first // CHUNK][:, places].bitcast(FP8X4),
                scales=h_planes[first // CHUNK][:, places],
                in_=h_bfs[index][:],
            )

        def product(bank, weight_cols, plane_cols, codes, plane, start, stop):
            nc.tensor.matmul_mx(
                out=bank,
                lhsT=w13_codes[:, weight_cols].bitcast(FP8X4),
                lhsT_scale=planes[:, plane_cols],
                rhs=codes,
                rhs_scale=plane,
                start=start,
                stop=stop,
            )

        w1_cols, w3_cols = slice(0, N), slice(N, 2 * N)
        tags = [f"acc{c}" for c in range(chunks - 1)] + ["h_bank0"]
        accs = [psum.tile([P, CHUNK], F32, name=f"acc{c}", tag=tags[c]) for c in range(chunks)]
        for c in range(chunks):
            product(accs[c][:], w1_cols, w1_plane_cols, *x_operand(c * CHUNK, CHUNK), True, False)
        result = keep.tile([P, S], F32, name="result")
        for c in range(chunks):
            product(accs[c][:], w3_cols, w3_plane_cols, h_codes[c][:].bitcast(FP8X4), h_planes[c][:], False, True)
            out_copy = nc.vector.tensor_copy if c >= chunks // 2 else nc.scalar.copy
            out_copy(result[:, c * CHUNK : (c + 1) * CHUNK], accs[c][:])

        for stored in (slice(0, 2 * CHUNK), slice(2 * CHUNK, S)):
            nc.sync.dma_start(out[:, stored], result[:, stored])
